import numpy as np
import ml_dtypes


def mxq(x, axis, fmt="e4m3"):
    dtype, down = {"e4m3": (ml_dtypes.float8_e4m3fn, 7), "e5m2": (ml_dtypes.float8_e5m2, 14)}[fmt]
    v = np.moveaxis(np.asarray(x, np.float32).astype(ml_dtypes.bfloat16).astype(np.float64), axis, -1)
    blocks = v.reshape(v.shape[:-1] + (-1, 32))
    amax = np.abs(blocks).max(-1, keepdims=True)
    byte = np.maximum(np.where(amax > 0, np.frexp(amax)[1] - 1 + 127, 0) - down, 1)
    scale = np.exp2(byte - 127.0)
    codes = (blocks / scale).astype(np.float32).astype(dtype).astype(np.float64)
    return np.moveaxis((codes * scale).reshape(v.shape), -1, axis)


WIDE = False


def mx_kscale(k):
    if not WIDE:
        return np.ones(k)
    levels = np.array([30, -30])
    if k % 512:
        return np.exp2(np.random.permutation(np.resize(levels, k // 32))).repeat(32)
    a = np.empty((k // 512, 16))
    for p in range(k // 512):
        a[p, :8] = np.random.permutation(np.resize(levels, 8))
        for g in range(8):
            far = levels[np.abs(levels - a[p, g]) >= 10]
            a[p, g + 8] = far[np.random.randint(len(far))]
    return np.exp2(a.ravel()).repeat(32)


def f64(x):
    return np.asarray(x).astype(np.float64)


K, M, T = 512, 2048, 1536


def setup_inputs():
    n = np.random.standard_normal
    s1 = mx_kscale(K)[:, None]
    s2 = mx_kscale(K)[:, None]
    return {
        "w": (n((K, M)) / np.sqrt(K) * s1).astype(np.float32),
        "xd": (n((K, T)) / s1).astype(np.float32),
        "wd": (n((K, M)) / np.sqrt(K) * s2).astype(np.float32),
        "x": (n((K, T)) / s2).astype(np.float32),
    }


def reference(w, xd, wd, x):
    w_ = mxq(f64(w), 0, "e4m3")
    xd_ = mxq(f64(xd), 0, "e5m2")
    wd_ = mxq(f64(wd), 0, "e5m2")
    x_ = mxq(f64(x), 0, "e4m3")
    y = w_.T @ xd_ + wd_.T @ x_
    return y

@@ -1,0 +1,184 @@
+from contextlib import ExitStack
+
+import concourse.mybir as mybir
+
+K, N, T = 512, 2048, 1536
+FLOPS = 2 * 2 * K * N * T
+
+F32 = mybir.dt.float32
+BF16 = mybir.dt.bfloat16
+U32 = mybir.dt.uint32
+U8 = mybir.dt.uint8
+E4M3 = mybir.dt.float8_e4m3fn_x4
+E5M2 = mybir.dt.float8_e5m2_x4
+
+P = 128
+PACK = 4
+T_TILE = 512
+T_TILES = T // T_TILE
+ROWS = 2
+BLOCK = P * ROWS
+BLOCKS = N // BLOCK
+WD_CHUNKS = (512, 512, 1024)
+
+
+def tile_mix_jvp_fm_none_kernel(tc, w, xd, wd, x, out):
+    nc = tc.nc
+    with ExitStack() as ctx:
+        keep = ctx.enter_context(tc.tile_pool(name="keep", bufs=1))
+        stage = ctx.enter_context(tc.tile_pool(name="stage", bufs=3))
+        results = ctx.enter_context(tc.tile_pool(name="results", bufs=5))
+        psum = ctx.enter_context(tc.psum_pool(name="psum", bufs=8))
+        ctx.enter_context(tc.manual_schedule())
+
+        def view(a):
+            return a.rearrange("(p j) c -> p j c", j=PACK)
+
+        x_raw = keep.tile([P, PACK, T], F32, name="x_raw")
+        nc.sync.dma_start(out=x_raw[:], in_=view(x))
+        xd_raw = keep.tile([P, PACK, T], F32, name="xd_raw")
+        nc.sync.dma_start(out=xd_raw[:], in_=view(xd))
+        w_raw = keep.tile([P, PACK, N], F32, name="w_raw")
+        nc.sync.dma_start(out=w_raw[:], in_=view(w))
+        wd_raw = []
+        c0 = 0
+        for width in WD_CHUNKS:
+            chunk = keep.tile([P, PACK, width], F32, name="wd_raw%d" % c0)
+            nc.sync.dma_start(out=chunk[:], in_=view(wd)[:, :, c0 : c0 + width])
+            for b in range(width // BLOCK):
+                wd_raw.append(chunk[:, :, b * BLOCK : (b + 1) * BLOCK])
+            c0 += width
+
+        x_codes = keep.tile([P, T], U32, name="x_codes", align_bytes=64)
+        x_scales = keep.tile([P, T], U8, name="x_scales", align_bytes=64)
+        xd_codes = keep.tile([P, T], U32, name="xd_codes", align_bytes=64)
+        xd_scales = keep.tile([P, T], U8, name="xd_scales", align_bytes=64)
+
+        def copy(engine, dst, src):
+            if engine == "v":
+                nc.vector.tensor_copy(out=dst, in_=src)
+            else:
+                nc.scalar.copy(out=dst, in_=src)
+
+        def prepare_moving(raw, codes, scales, fmt):
+            staged = {}
+            for c, engine in ((0, "v"), (1, "s"), (2, "v")):
+                g = stage.tile([P, T_TILE, PACK], BF16, name="g", align_bytes=64)
+                copy(
+                    engine,
+                    g[:].rearrange("p (c i) j -> p c j i", i=4),
+                    raw[:, :, c * T_TILE : (c + 1) * T_TILE].rearrange("p j (c i) -> p c j i", i=4),
+                )
+                staged[c] = g
+            for c in (0, 2, 1):
+                cols = slice(c * T_TILE, (c + 1) * T_TILE)
+                nc.vector.quantize_mx(
+                    out=codes[:, cols].bitcast(fmt),
+                    scales=scales[:, cols],
+                    in_=staged[c][:].rearrange("p c j -> p (c j)"),
+                )
+
+        w_staged, wd_staged, w_mx, wd_mx = {}, {}, {}, {}
+
+        def stage_stationary(b, engine, src, staged):
+            s = stage.tile([P, ROWS, P, PACK], BF16, name="s", bufs=5, align_bytes=64)
+            copy(
+                engine,
+                s[:].rearrange("p i m j -> p m j i"),
+                src.rearrange("p j (m i) -> p m j i", i=ROWS),
+            )
+            staged[b] = s
+
+        def stage_w(b, engine):
+            stage_stationary(b, engine, w_raw[:, :, b * BLOCK : (b + 1) * BLOCK], w_staged)
+
+        def stage_wd(b, engine):
+            stage_stationary(b, engine, wd_raw[b], wd_staged)
+
+        def quantise_stationary(b, staged, mx, fmt, label):
+            codes = keep.tile([P, BLOCK], U32, name="%s_codes%d" % (label, b), align_bytes=64)
+            scales = keep.tile([P, BLOCK], U8, name="%s_scales%d" % (label, b), align_bytes=64)
+            nc.vector.quantize_mx(
+                out=codes[:].bitcast(fmt),
+                scales=scales[:],
+                in_=staged[b][:].rearrange("p i m j -> p (i m j)"),
+            )
+            mx[b] = (codes, scales)
+
+        def quantise_w(b):
+            quantise_stationary(b, w_staged, w_mx, E4M3, "w")
+
+        def quantise_wd(b):
+            quantise_stationary(b, wd_staged, wd_mx, E5M2, "wd")
+
+        banks = {}
+
+        def multiply(b, i, second):
+            codes, scales = wd_mx[b] if second else w_mx[b]
+            for c in range(T_TILES):
+                if not second:
+                    acc = psum.tile([P, T_TILE], F32, name="acc")
+                    banks[b, i, c] = acc
+                t_cols = slice(c * T_TILE, (c + 1) * T_TILE)
+                n_cols = slice(i * P, (i + 1) * P)
+                nc.tensor.matmul_mx(
+                    out=banks[b, i, c][:],
+                    lhsT=codes[:, n_cols].bitcast(E5M2 if second else E4M3),
+                    lhsT_scale=scales[:, n_cols],
+                    rhs=(x_codes if second else xd_codes)[:, t_cols].bitcast(E4M3 if second else E5M2),
+                    rhs_scale=(x_scales if second else xd_scales)[:, t_cols],
+                    start=not second,
+                    stop=second,
+                )
+
+        prepare_moving(x_raw, x_codes, x_scales, E4M3)
+        prepare_moving(xd_raw, xd_codes, xd_scales, E5M2)
+
+        stage_w(0, "v")
+        stage_w(1, "s")
+        stage_w(2, "v")
+        quantise_w(0)
+        quantise_w(1)
+        multiply(0, 0, False)
+        multiply(0, 1, False)
+        stage_w(3, "s")
+        stage_wd(0, "v")
+        stage_wd(1, "s")
+        quantise_w(2)
+        quantise_wd(0)
+        multiply(0, 0, True)
+        multiply(0, 1, True)
+        quantise_wd(1)
+        quantise_w(3)
+
+        steps = {
+            (0, 1): [lambda: stage_wd(2, "v")],
+            (0, 3): [lambda: stage_wd(3, "v"), lambda: quantise_wd(2)],
+            (0, 5): [lambda: quantise_wd(3)],
+        }
+        for b in range(1, 5):
+            steps[b, 0] = [lambda b=b: stage_w(b + 3, "v"), lambda b=b: stage_wd(b + 3, "v")]
+            steps[b, 2] = [lambda b=b: quantise_w(b + 3)]
+            steps[b, 4] = [lambda b=b: quantise_wd(b + 3)]
+        vector_banks = {0: (2, 5), 1: (3,), 2: (3,), 3: (3,), 4: (1, 4), 5: (1, 3, 5), 6: (1, 3, 5), 7: (1, 3, 5)}
+
+        out_view = out.rearrange("(b m i) t -> b m i t", m=P, i=ROWS)
+        for b in range(BLOCKS):
+            result = results.tile([P, ROWS, T], F32, name="result")
+            for i in range(ROWS):
+                if b > 0:
+                    multiply(b, i, False)
+                    multiply(b, i, True)
+                for c in range(T_TILES):
+                    q = i * T_TILES + c
+                    copy(
+                        "v" if q in vector_banks[b] else "s",
+                        result[:, i, c * T_TILE : (c + 1) * T_TILE],
+                        banks[b, i, c][:],
+                    )
+                    for step in steps.get((b, q), []):
+                        step()
+                if b in (0, BLOCKS - 1):
+                    nc.sync.dma_start(out=out_view[b][:, i : i + 1, :], in_=result[:, i : i + 1, :])
+            if b not in (0, BLOCKS - 1):
+                nc.sync.dma_start(out=out_view[b], in_=result[:])

@@ -19,7 +19,8 @@ T_TILES = T // T_TILE
 ROWS = 2
 BLOCK = P * ROWS
 BLOCKS = N // BLOCK
-WD_CHUNKS = (512, 512, 1024)
+WD_CHUNKS = (512, 1536)
+WARM_UP = 12
 
 
 def tile_mix_jvp_fm_none_kernel(tc, w, xd, wd, x, out):
@@ -113,10 +114,12 @@ def tile_mix_jvp_fm_none_kernel(tc, w, xd, wd, x, out):
 
         banks = {}
 
-        def multiply(b, i, second):
+        def multiply(b, i, second, t_tiles=range(T_TILES)):
             codes, scales = wd_mx[b] if second else w_mx[b]
-            for c in range(T_TILES):
+            for c in t_tiles:
                 if not second:
+                    if (b, i, c) in banks:
+                        continue
                     acc = psum.tile([P, T_TILE], F32, name="acc")
                     banks[b, i, c] = acc
                 t_cols = slice(c * T_TILE, (c + 1) * T_TILE)
@@ -134,13 +137,26 @@ def tile_mix_jvp_fm_none_kernel(tc, w, xd, wd, x, out):
         prepare_moving(x_raw, x_codes, x_scales, E4M3)
         prepare_moving(xd_raw, xd_codes, xd_scales, E5M2)
 
+        idle = psum.tile([P, T_TILE], F32, name="acc")
+        for n in range(WARM_UP):
+            nc.tensor.matmul_mx(
+                out=idle[:],
+                lhsT=x_codes[:, :P].bitcast(E4M3),
+                lhsT_scale=x_scales[:, :P],
+                rhs=xd_codes[:, T_TILE : 2 * T_TILE].bitcast(E5M2),
+                rhs_scale=xd_scales[:, T_TILE : 2 * T_TILE],
+                start=True,
+                stop=True,
+            )
+
         stage_w(0, "v")
         stage_w(1, "s")
-        stage_w(2, "v")
         quantise_w(0)
+        stage_w(2, "v")
         quantise_w(1)
         multiply(0, 0, False)
         multiply(0, 1, False)
+        multiply(1, 0, False, range(2))
         stage_w(3, "s")
         stage_wd(0, "v")
         stage_wd(1, "s")
@@ -152,15 +168,24 @@ def tile_mix_jvp_fm_none_kernel(tc, w, xd, wd, x, out):
         quantise_w(3)
 
         steps = {
-            (0, 1): [lambda: stage_wd(2, "v")],
-            (0, 3): [lambda: stage_wd(3, "v"), lambda: quantise_wd(2)],
-            (0, 5): [lambda: quantise_wd(3)],
+            (0, 5): [lambda: stage_w(4, "v"), lambda: stage_w(5, "v"), lambda: quantise_w(4)],
+            (1, 2): [lambda: quantise_w(5)],
+            (1, 5): [
+                lambda: multiply(2, 0, False),
+                lambda: multiply(2, 1, False),
+                lambda: multiply(3, 0, False, range(2)),
+                lambda: stage_wd(2, "v"),
+                lambda: quantise_wd(2),
+                lambda: stage_wd(3, "v"),
+            ],
+            (2, 0): [lambda: stage_w(6, "v"), lambda: quantise_wd(3)],
+            (3, 0): [lambda: stage_w(7, "v"), lambda: quantise_w(6)],
+            (4, 1): [lambda: quantise_w(7)],
         }
-        for b in range(1, 5):
-            steps[b, 0] = [lambda b=b: stage_w(b + 3, "v"), lambda b=b: stage_wd(b + 3, "v")]
-            steps[b, 2] = [lambda b=b: quantise_w(b + 3)]
-            steps[b, 4] = [lambda b=b: quantise_wd(b + 3)]
-        vector_banks = {0: (2, 5), 1: (3,), 2: (3,), 3: (3,), 4: (1, 4), 5: (1, 3, 5), 6: (1, 3, 5), 7: (1, 3, 5)}
+        for b in range(2, 6):
+            steps[b, 3] = [lambda b=b: stage_wd(b + 2, "v")]
+            steps[b, 4] = [lambda b=b: quantise_wd(b + 2)]
+        vector_banks = {0: (1, 3, 5), 1: (2,), 2: (3,), 3: (3,), 4: (1, 4), 5: (1, 4), 6: (1, 3, 5), 7: (1, 3, 5)}
 
         out_view = out.rearrange("(b m i) t -> b m i t", m=P, i=ROWS)
         for b in range(BLOCKS):
@@ -178,7 +203,7 @@ def tile_mix_jvp_fm_none_kernel(tc, w, xd, wd, x, out):
                     )
                     for step in steps.get((b, q), []):
                         step()
-                if b in (0, BLOCKS - 1):
+                if b == BLOCKS - 1:
                     nc.sync.dma_start(out=out_view[b][:, i : i + 1, :], in_=result[:, i : i + 1, :])
-            if b not in (0, BLOCKS - 1):
+            if b < BLOCKS - 1:
                 nc.sync.dma_start(out=out_view[b], in_=result[:])

@@ -35,16 +35,16 @@ def tile_mix_jvp_fm_none_kernel(tc, w, xd, wd, x, out):
         def view(a):
             return a.rearrange("(p j) c -> p j c", j=PACK)
 
-        x_raw = keep.tile([P, PACK, T], F32, name="x_raw")
+        x_raw = keep.tile([P, PACK, T], F32, name="x_raw", align_bytes=256)
         nc.sync.dma_start(out=x_raw[:], in_=view(x))
-        xd_raw = keep.tile([P, PACK, T], F32, name="xd_raw")
+        xd_raw = keep.tile([P, PACK, T], F32, name="xd_raw", align_bytes=256)
         nc.sync.dma_start(out=xd_raw[:], in_=view(xd))
-        w_raw = keep.tile([P, PACK, N], F32, name="w_raw")
+        w_raw = keep.tile([P, PACK, N], F32, name="w_raw", align_bytes=256)
         nc.sync.dma_start(out=w_raw[:], in_=view(w))
         wd_raw = []
         c0 = 0
         for width in WD_CHUNKS:
-            chunk = keep.tile([P, PACK, width], F32, name="wd_raw%d" % c0)
+            chunk = keep.tile([P, PACK, width], F32, name="wd_raw%d" % c0, align_bytes=256)
             nc.sync.dma_start(out=chunk[:], in_=view(wd)[:, :, c0 : c0 + width])
             for b in range(width // BLOCK):
                 wd_raw.append(chunk[:, :, b * BLOCK : (b + 1) * BLOCK])
@@ -189,7 +189,7 @@ def tile_mix_jvp_fm_none_kernel(tc, w, xd, wd, x, out):
 
         out_view = out.rearrange("(b m i) t -> b m i t", m=P, i=ROWS)
         for b in range(BLOCKS):
-            result = results.tile([P, ROWS, T], F32, name="result")
+            result = results.tile([P, ROWS, T], F32, name="result", align_bytes=256)
             for i in range(ROWS):
                 if b > 0:
                     multiply(b, i, False)

@@ -16,39 +16,37 @@ P = 128
 PACK = 4
 T_TILE = 512
 T_TILES = T // T_TILE
-ROWS = 2
-BLOCK = P * ROWS
+BLOCK = 2 * P
 BLOCKS = N // BLOCK
-WD_CHUNKS = (512, 1536)
-WARM_UP = 12
+EARLY = 512
+FIRST_LATE = EARLY // BLOCK
+SINGLE = (0, FIRST_LATE)
+DMA_ALIGN = 256
+ROW_BYTES = 4 * T
 
 
 def tile_mix_jvp_fm_none_kernel(tc, w, xd, wd, x, out):
     nc = tc.nc
     with ExitStack() as ctx:
+        shared = ctx.enter_context(tc.tile_pool(name="shared", bufs=1))
         keep = ctx.enter_context(tc.tile_pool(name="keep", bufs=1))
         stage = ctx.enter_context(tc.tile_pool(name="stage", bufs=3))
-        results = ctx.enter_context(tc.tile_pool(name="results", bufs=5))
         psum = ctx.enter_context(tc.psum_pool(name="psum", bufs=8))
         ctx.enter_context(tc.manual_schedule())
 
         def view(a):
             return a.rearrange("(p j) c -> p j c", j=PACK)
 
-        x_raw = keep.tile([P, PACK, T], F32, name="x_raw", align_bytes=256)
+        x_raw = shared.tile([P, PACK, T], F32, name="x_raw", align_bytes=DMA_ALIGN, offset=0)
         nc.sync.dma_start(out=x_raw[:], in_=view(x))
-        xd_raw = keep.tile([P, PACK, T], F32, name="xd_raw", align_bytes=256)
+        xd_raw = shared.tile([P, PACK, T], F32, name="xd_raw", align_bytes=DMA_ALIGN, offset=PACK * ROW_BYTES)
         nc.sync.dma_start(out=xd_raw[:], in_=view(xd))
-        w_raw = keep.tile([P, PACK, N], F32, name="w_raw", align_bytes=256)
+        wd_early = keep.tile([P, PACK, EARLY], F32, name="wd_early", align_bytes=DMA_ALIGN)
+        nc.sync.dma_start(out=wd_early[:], in_=view(wd)[:, :, :EARLY])
+        w_raw = keep.tile([P, PACK, N], F32, name="w_raw", align_bytes=DMA_ALIGN)
         nc.sync.dma_start(out=w_raw[:], in_=view(w))
-        wd_raw = []
-        c0 = 0
-        for width in WD_CHUNKS:
-            chunk = keep.tile([P, PACK, width], F32, name="wd_raw%d" % c0, align_bytes=256)
-            nc.sync.dma_start(out=chunk[:], in_=view(wd)[:, :, c0 : c0 + width])
-            for b in range(width // BLOCK):
-                wd_raw.append(chunk[:, :, b * BLOCK : (b + 1) * BLOCK])
-            c0 += width
+        wd_late = keep.tile([P, PACK, N - EARLY], F32, name="wd_late", align_bytes=DMA_ALIGN)
+        nc.sync.dma_start(out=wd_late[:], in_=view(wd)[:, :, EARLY:])
 
         x_codes = keep.tile([P, T], U32, name="x_codes", align_bytes=64)
         x_scales = keep.tile([P, T], U8, name="x_scales", align_bytes=64)
@@ -61,149 +59,197 @@ def tile_mix_jvp_fm_none_kernel(tc, w, xd, wd, x, out):
             else:
                 nc.scalar.copy(out=dst, in_=src)
 
-        def prepare_moving(raw, codes, scales, fmt):
-            staged = {}
-            for c, engine in ((0, "v"), (1, "s"), (2, "v")):
-                g = stage.tile([P, T_TILE, PACK], BF16, name="g", align_bytes=64)
-                copy(
-                    engine,
-                    g[:].rearrange("p (c i) j -> p c j i", i=4),
-                    raw[:, :, c * T_TILE : (c + 1) * T_TILE].rearrange("p j (c i) -> p c j i", i=4),
-                )
-                staged[c] = g
-            for c in (0, 2, 1):
-                cols = slice(c * T_TILE, (c + 1) * T_TILE)
-                nc.vector.quantize_mx(
-                    out=codes[:, cols].bitcast(fmt),
-                    scales=scales[:, cols],
-                    in_=staged[c][:].rearrange("p c j -> p (c j)"),
-                )
-
-        w_staged, wd_staged, w_mx, wd_mx = {}, {}, {}, {}
-
-        def stage_stationary(b, engine, src, staged):
-            s = stage.tile([P, ROWS, P, PACK], BF16, name="s", bufs=5, align_bytes=64)
+        def interleave(engine, dst, src):
             copy(
                 engine,
-                s[:].rearrange("p i m j -> p m j i"),
-                src.rearrange("p j (m i) -> p m j i", i=ROWS),
+                dst.rearrange("p (c i) j -> p c j i", i=4),
+                src.rearrange("p j (c i) -> p c j i", i=4),
             )
-            staged[b] = s
 
-        def stage_w(b, engine):
-            stage_stationary(b, engine, w_raw[:, :, b * BLOCK : (b + 1) * BLOCK], w_staged)
+        def stage_moving(raw, c, engine):
+            g = stage.tile([P, T_TILE, PACK], BF16, name="g", align_bytes=64)
+            interleave(engine, g[:], raw[:, :, c * T_TILE : (c + 1) * T_TILE])
+            return g
 
-        def stage_wd(b, engine):
-            stage_stationary(b, engine, wd_raw[b], wd_staged)
-
-        def quantise_stationary(b, staged, mx, fmt, label):
-            codes = keep.tile([P, BLOCK], U32, name="%s_codes%d" % (label, b), align_bytes=64)
-            scales = keep.tile([P, BLOCK], U8, name="%s_scales%d" % (label, b), align_bytes=64)
+        def quantise_moving(tiles, c, codes, scales, fmt):
+            cols = slice(c * T_TILE, (c + 1) * T_TILE)
             nc.vector.quantize_mx(
-                out=codes[:].bitcast(fmt),
-                scales=scales[:],
-                in_=staged[b][:].rearrange("p i m j -> p (i m j)"),
+                out=codes[:, cols].bitcast(fmt),
+                scales=scales[:, cols],
+                in_=tiles[c][:].rearrange("p c j -> p (c j)"),
             )
-            mx[b] = (codes, scales)
 
-        def quantise_w(b):
-            quantise_stationary(b, w_staged, w_mx, E4M3, "w")
+        def raw_columns(name, c0, width):
+            if name == "w":
+                return w_raw[:, :, c0 : c0 + width]
+            if c0 < EARLY:
+                return wd_early[:, :, c0 : c0 + width]
+            return wd_late[:, :, c0 - EARLY : c0 - EARLY + width]
 
-        def quantise_wd(b):
-            quantise_stationary(b, wd_staged, wd_mx, E5M2, "wd")
+        staged, mx = {}, {}
 
-        banks = {}
+        def stage_tile(name, tile):
+            s = stage.tile([P, P, PACK], BF16, name="s1", bufs=2, align_bytes=64)
+            interleave("v", s[:], raw_columns(name, tile * P, P))
+            staged[name, tile] = s[:].rearrange("p m j -> p (m j)")
 
-        def multiply(b, i, second, t_tiles=range(T_TILES)):
-            codes, scales = wd_mx[b] if second else w_mx[b]
-            for c in t_tiles:
-                if not second:
-                    if (b, i, c) in banks:
-                        continue
-                    acc = psum.tile([P, T_TILE], F32, name="acc")
-                    banks[b, i, c] = acc
-                t_cols = slice(c * T_TILE, (c + 1) * T_TILE)
-                n_cols = slice(i * P, (i + 1) * P)
-                nc.tensor.matmul_mx(
-                    out=banks[b, i, c][:],
-                    lhsT=codes[:, n_cols].bitcast(E5M2 if second else E4M3),
-                    lhsT_scale=scales[:, n_cols],
-                    rhs=(x_codes if second else xd_codes)[:, t_cols].bitcast(E4M3 if second else E5M2),
-                    rhs_scale=(x_scales if second else xd_scales)[:, t_cols],
-                    start=not second,
-                    stop=second,
+        def stage_block(name, b, engine):
+            s = stage.tile([P, BLOCK, PACK], BF16, name="s2", bufs=4, align_bytes=64)
+            src = raw_columns(name, b * BLOCK, BLOCK)
+            if b in SINGLE:
+                interleave(engine, s[:], src)
+            else:
+                copy(
+                    engine,
+                    s[:].rearrange("p (i c h) j -> p c j h i", i=2, h=2),
+                    src.rearrange("p j (c h i) -> p c j h i", i=2, h=2),
                 )
+            staged[name, 2 * b] = s[:].rearrange("p m j -> p (m j)")
 
-        prepare_moving(x_raw, x_codes, x_scales, E4M3)
-        prepare_moving(xd_raw, xd_codes, xd_scales, E5M2)
+        def quantise(name, tile, tiles):
+            codes = keep.tile([P, tiles * P], U32, name="%s_codes%d" % (name, tile), align_bytes=64)
+            scales = keep.tile([P, tiles * P], U8, name="%s_scales%d" % (name, tile), align_bytes=64)
+            nc.vector.quantize_mx(
+                out=codes[:].bitcast(E4M3 if name == "w" else E5M2),
+                scales=scales[:],
+                in_=staged[name, tile],
+            )
+            for i in range(tiles):
+                mx[name, tile + i] = (codes[:, i * P : (i + 1) * P], scales[:, i * P : (i + 1) * P])
 
-        idle = psum.tile([P, T_TILE], F32, name="acc")
-        for n in range(WARM_UP):
+        def quantise_block(name, b):
+            quantise(name, 2 * b, 2)
+
+        def first_tiles(name, b):
+            stage_tile(name, 2 * b)
+            stage_tile(name, 2 * b + 1)
+            quantise(name, 2 * b, 1)
+            quantise(name, 2 * b + 1, 1)
+
+        banks, parked, results = {}, set(), {}
+
+        def result(b):
+            if b not in results:
+                results[b] = shared.tile(
+                    [P, 2, T], F32, name="result%d" % b, align_bytes=DMA_ALIGN, offset=2 * b * ROW_BYTES
+                )
+            return results[b]
+
+        def target(tile, c):
+            return result(tile // 2)[:, tile % 2, c * T_TILE : (c + 1) * T_TILE]
+
+        def one_pass(name, tile, c, start, stop):
+            codes, scales = mx[name, tile]
+            if start:
+                banks[tile, c] = psum.tile([P, T_TILE], F32, name="acc")
+            cols = slice(c * T_TILE, (c + 1) * T_TILE)
             nc.tensor.matmul_mx(
-                out=idle[:],
-                lhsT=x_codes[:, :P].bitcast(E4M3),
-                lhsT_scale=x_scales[:, :P],
-                rhs=xd_codes[:, T_TILE : 2 * T_TILE].bitcast(E5M2),
-                rhs_scale=xd_scales[:, T_TILE : 2 * T_TILE],
-                start=True,
-                stop=True,
+                out=banks[tile, c][:],
+                lhsT=codes.bitcast(E4M3 if name == "w" else E5M2),
+                lhsT_scale=scales,
+                rhs=(xd_codes if name == "w" else x_codes)[:, cols].bitcast(E5M2 if name == "w" else E4M3),
+                rhs_scale=(xd_scales if name == "w" else x_scales)[:, cols],
+                start=start,
+                stop=stop,
             )
 
-        stage_w(0, "v")
-        stage_w(1, "s")
-        quantise_w(0)
-        stage_w(2, "v")
-        quantise_w(1)
-        multiply(0, 0, False)
-        multiply(0, 1, False)
-        multiply(1, 0, False, range(2))
-        stage_w(3, "s")
-        stage_wd(0, "v")
-        stage_wd(1, "s")
-        quantise_w(2)
-        quantise_wd(0)
-        multiply(0, 0, True)
-        multiply(0, 1, True)
-        quantise_wd(1)
-        quantise_w(3)
+        def first_name(tile):
+            return "wd" if tile * P < EARLY else "w"
 
-        steps = {
-            (0, 5): [lambda: stage_w(4, "v"), lambda: stage_w(5, "v"), lambda: quantise_w(4)],
-            (1, 2): [lambda: quantise_w(5)],
-            (1, 5): [
-                lambda: multiply(2, 0, False),
-                lambda: multiply(2, 1, False),
-                lambda: multiply(3, 0, False, range(2)),
-                lambda: stage_wd(2, "v"),
-                lambda: quantise_wd(2),
-                lambda: stage_wd(3, "v"),
+        def second_name(tile):
+            return "w" if tile * P < EARLY else "wd"
+
+        def open_banks(tile, t_tiles=range(T_TILES)):
+            for c in t_tiles:
+                if (tile, c) not in banks:
+                    one_pass(first_name(tile), tile, c, True, False)
+
+        def close_banks(tile):
+            for c in range(T_TILES):
+                one_pass(second_name(tile), tile, c, (tile, c) in parked, True)
+
+        def park_pass(tile, c):
+            one_pass(first_name(tile), tile, c, True, True)
+            parked.add((tile, c))
+
+        def park_copy(tile, c, engine):
+            copy(engine, target(tile, c), banks[tile, c][:])
+
+        def empty(tile, c, engine):
+            if (tile, c) in parked:
+                nc.vector.tensor_tensor(
+                    out=target(tile, c), in0=banks[tile, c][:], in1=target(tile, c), op=mybir.AluOpType.add
+                )
+            else:
+                copy(engine, target(tile, c), banks[tile, c][:])
+
+        x_staged = [stage_moving(x_raw, c, engine) for c, engine in enumerate("vsv")]
+        for c in (0, 2, 1):
+            quantise_moving(x_staged, c, x_codes, x_scales, E4M3)
+        xd_staged = [stage_moving(xd_raw, c, "s") for c in range(T_TILES - 1)]
+        stage_block("wd", 1, "s")
+        xd_staged.append(stage_moving(xd_raw, T_TILES - 1, "s"))
+        stage_block("wd", 0, "v")
+        quantise_moving(xd_staged, 0, xd_codes, xd_scales, E5M2)
+        quantise_moving(xd_staged, 1, xd_codes, xd_scales, E5M2)
+        quantise_block("wd", 1)
+        for c in range(T_TILES):
+            park_pass(3, c)
+        park_pass(2, 2)
+        open_banks(2)
+        park_copy(3, 0, "v")
+        park_copy(3, 1, "v")
+        park_copy(3, 2, "v")
+        quantise_moving(xd_staged, 2, xd_codes, xd_scales, E5M2)
+        quantise_block("wd", 0)
+        park_copy(2, 2, "v")
+        open_banks(0)
+        open_banks(1)
+
+        first_tiles("w", 0)
+        stage_block("w", 3, "s")
+        stage_block("w", 1, "v")
+        quantise_block("w", 3)
+        quantise_block("w", 1)
+
+        def run_ahead():
+            for c in range(T_TILES):
+                park_pass(7, c)
+            for c in range(T_TILES):
+                park_copy(7, c, "s")
+            open_banks(4)
+            open_banks(5)
+            open_banks(6, range(2))
+
+        after = {
+            0: [lambda: stage_block("w", 2, "v"), lambda: quantise_block("w", 2)],
+            3: [
+                run_ahead,
+                lambda: first_tiles("wd", 2),
+                lambda: stage_block("wd", 3, "v"),
+                lambda: stage_block("w", 4, "s"),
             ],
-            (2, 0): [lambda: stage_w(6, "v"), lambda: quantise_wd(3)],
-            (3, 0): [lambda: stage_w(7, "v"), lambda: quantise_w(6)],
-            (4, 1): [lambda: quantise_w(7)],
+            4: [lambda: quantise_block("wd", 3), lambda: stage_block("wd", 4, "v"), lambda: quantise_block("w", 4)],
+            5: [lambda: stage_block("w", 5, "v"), lambda: quantise_block("wd", 4)],
         }
-        for b in range(2, 6):
-            steps[b, 3] = [lambda b=b: stage_wd(b + 2, "v")]
-            steps[b, 4] = [lambda b=b: quantise_wd(b + 2)]
-        vector_banks = {0: (1, 3, 5), 1: (2,), 2: (3,), 3: (3,), 4: (1, 4), 5: (1, 4), 6: (1, 3, 5), 7: (1, 3, 5)}
+        for b in range(5, BLOCKS):
+            after[2 * b - 3] = [lambda b=b: quantise_block("w", b), lambda b=b: stage_block("wd", b, "v")]
+            after[2 * b - 2] = [lambda b=b: quantise_block("wd", b)]
+            if b + 1 < BLOCKS:
+                after[2 * b - 2].append(lambda b=b: stage_block("w", b + 1, "v"))
+        scalar_alone = (1, 5, 6)
 
-        out_view = out.rearrange("(b m i) t -> b m i t", m=P, i=ROWS)
         for b in range(BLOCKS):
-            result = results.tile([P, ROWS, T], F32, name="result", align_bytes=256)
-            for i in range(ROWS):
-                if b > 0:
-                    multiply(b, i, False)
-                    multiply(b, i, True)
+            rows = out[b * BLOCK : (b + 1) * BLOCK, :]
+            for i in range(2):
+                tile = 2 * b + i
+                open_banks(tile)
+                close_banks(tile)
                 for c in range(T_TILES):
-                    q = i * T_TILES + c
-                    copy(
-                        "v" if q in vector_banks[b] else "s",
-                        result[:, i, c * T_TILE : (c + 1) * T_TILE],
-                        banks[b, i, c][:],
-                    )
-                    for step in steps.get((b, q), []):
-                        step()
-                if b == BLOCKS - 1:
-                    nc.sync.dma_start(out=out_view[b][:, i : i + 1, :], in_=result[:, i : i + 1, :])
-            if b < BLOCKS - 1:
-                nc.sync.dma_start(out=out_view[b], in_=result[:])
+                    empty(tile, c, "v" if c == T_TILES - 1 and tile not in scalar_alone else "s")
+                for step in after.get(tile, []):
+                    step()
+                if b in SINGLE:
+                    nc.sync.dma_start(out=rows[i * P : (i + 1) * P, :], in_=result(b)[:, i, :])
+            if b not in SINGLE:
+                nc.sync.dma_start(out=rows.rearrange("(m i) t -> m i t", i=2), in_=result(b)[:])

@@ -42,7 +42,7 @@ def tile_mix_jvp_fm_none_kernel(tc, w, xd, wd, x, out):
         xd_raw = shared.tile([P, PACK, T], F32, name="xd_raw", align_bytes=DMA_ALIGN, offset=PACK * ROW_BYTES)
         nc.sync.dma_start(out=xd_raw[:], in_=view(xd))
         wd_early = keep.tile([P, PACK, EARLY], F32, name="wd_early", align_bytes=DMA_ALIGN)
-        nc.sync.dma_start(out=wd_early[:], in_=view(wd)[:, :, :EARLY])
+        nc.scalar.dma_start(out=wd_early[:], in_=view(wd)[:, :, :EARLY])
         w_raw = keep.tile([P, PACK, N], F32, name="w_raw", align_bytes=DMA_ALIGN)
         nc.sync.dma_start(out=w_raw[:], in_=view(w))
         wd_late = keep.tile([P, PACK, N - EARLY], F32, name="wd_late", align_bytes=DMA_ALIGN)

@@ -39,10 +39,10 @@ def tile_mix_jvp_fm_none_kernel(tc, w, xd, wd, x, out):
 
         x_raw = shared.tile([P, PACK, T], F32, name="x_raw", align_bytes=DMA_ALIGN, offset=0)
         nc.sync.dma_start(out=x_raw[:], in_=view(x))
-        xd_raw = shared.tile([P, PACK, T], F32, name="xd_raw", align_bytes=DMA_ALIGN, offset=PACK * ROW_BYTES)
-        nc.sync.dma_start(out=xd_raw[:], in_=view(xd))
         wd_early = keep.tile([P, PACK, EARLY], F32, name="wd_early", align_bytes=DMA_ALIGN)
         nc.scalar.dma_start(out=wd_early[:], in_=view(wd)[:, :, :EARLY])
+        xd_raw = shared.tile([P, PACK, T], F32, name="xd_raw", align_bytes=DMA_ALIGN, offset=PACK * ROW_BYTES)
+        nc.sync.dma_start(out=xd_raw[:], in_=view(xd))
         w_raw = keep.tile([P, PACK, N], F32, name="w_raw", align_bytes=DMA_ALIGN)
         nc.sync.dma_start(out=w_raw[:], in_=view(w))
         wd_late = keep.tile([P, PACK, N - EARLY], F32, name="wd_late", align_bytes=DMA_ALIGN)
@@ -186,7 +186,7 @@ def tile_mix_jvp_fm_none_kernel(tc, w, xd, wd, x, out):
         x_staged = [stage_moving(x_raw, c, engine) for c, engine in enumerate("vsv")]
         for c in (0, 2, 1):
             quantise_moving(x_staged, c, x_codes, x_scales, E4M3)
-        xd_staged = [stage_moving(xd_raw, c, "s") for c in range(T_TILES - 1)]
+        xd_staged = [stage_moving(xd_raw, c, engine) for c, engine in enumerate("sv")]
         stage_block("wd", 1, "s")
         xd_staged.append(stage_moving(xd_raw, T_TILES - 1, "s"))
         stage_block("wd", 0, "v")

@@ -14,21 +14,23 @@ E5M2 = mybir.dt.float8_e5m2_x4
 
 P = 128
 PACK = 4
-T_TILE = 512
-T_TILES = T // T_TILE
-BLOCK = 2 * P
-BLOCKS = N // BLOCK
-EARLY = 512
-FIRST_LATE = EARLY // BLOCK
-SINGLE = (0, FIRST_LATE)
+BANK = 512
+THIRDS = T // BANK
+TILES = N // P
+EARLY_TILES = 6
+LATE_TILES = TILES - EARLY_TILES
+EARLY = EARLY_TILES * P
 DMA_ALIGN = 256
 ROW_BYTES = 4 * T
+EARLY_STORES = (5, 6, 7)
+LATE_STORES = (10, 10, 10)
 
 
 def tile_mix_jvp_fm_none_kernel(tc, w, xd, wd, x, out):
     nc = tc.nc
     with ExitStack() as ctx:
         shared = ctx.enter_context(tc.tile_pool(name="shared", bufs=1))
+        late = ctx.enter_context(tc.tile_pool(name="late", bufs=1))
         keep = ctx.enter_context(tc.tile_pool(name="keep", bufs=1))
         stage = ctx.enter_context(tc.tile_pool(name="stage", bufs=3))
         psum = ctx.enter_context(tc.psum_pool(name="psum", bufs=8))
@@ -37,21 +39,22 @@ def tile_mix_jvp_fm_none_kernel(tc, w, xd, wd, x, out):
         def view(a):
             return a.rearrange("(p j) c -> p j c", j=PACK)
 
-        x_raw = shared.tile([P, PACK, T], F32, name="x_raw", align_bytes=DMA_ALIGN, offset=0)
-        nc.sync.dma_start(out=x_raw[:], in_=view(x))
-        wd_early = keep.tile([P, PACK, EARLY], F32, name="wd_early", align_bytes=DMA_ALIGN)
-        nc.scalar.dma_start(out=wd_early[:], in_=view(wd)[:, :, :EARLY])
-        xd_raw = shared.tile([P, PACK, T], F32, name="xd_raw", align_bytes=DMA_ALIGN, offset=PACK * ROW_BYTES)
+        xd_raw = shared.tile([P, PACK, T], F32, name="xd_raw", align_bytes=DMA_ALIGN, offset=0)
         nc.sync.dma_start(out=xd_raw[:], in_=view(xd))
-        w_raw = keep.tile([P, PACK, N], F32, name="w_raw", align_bytes=DMA_ALIGN)
-        nc.sync.dma_start(out=w_raw[:], in_=view(w))
-        wd_late = keep.tile([P, PACK, N - EARLY], F32, name="wd_late", align_bytes=DMA_ALIGN)
-        nc.sync.dma_start(out=wd_late[:], in_=view(wd)[:, :, EARLY:])
+        w_early = keep.tile([P, PACK, EARLY], F32, name="w_early", align_bytes=DMA_ALIGN)
+        nc.gpsimd.dma_start(out=w_early[:], in_=view(w)[:, :, :EARLY])
+        x_raw = shared.tile([P, PACK, T], F32, name="x_raw", align_bytes=DMA_ALIGN, offset=EARLY_TILES * ROW_BYTES)
+        nc.gpsimd.dma_start(out=x_raw[:], in_=view(x))
+        wd_raw = keep.tile([P, PACK, N], F32, name="wd_raw", align_bytes=DMA_ALIGN)
+        nc.gpsimd.dma_start(out=wd_raw[:], in_=view(wd))
 
-        x_codes = keep.tile([P, T], U32, name="x_codes", align_bytes=64)
-        x_scales = keep.tile([P, T], U8, name="x_scales", align_bytes=64)
-        xd_codes = keep.tile([P, T], U32, name="xd_codes", align_bytes=64)
-        xd_scales = keep.tile([P, T], U8, name="xd_scales", align_bytes=64)
+        moving = {}
+        for name in ("xd", "x"):
+            codes = keep.tile([P, T], U32, name=name + "_codes", align_bytes=64)
+            scales = keep.tile([P, T], U8, name=name + "_scales", align_bytes=64)
+            moving[name] = (codes, scales)
+        fmt = {"w": E4M3, "x": E4M3, "wd": E5M2, "xd": E5M2}
+        partner = {"w": "xd", "wd": "x"}
 
         def copy(engine, dst, src):
             if engine == "v":
@@ -59,197 +62,201 @@ def tile_mix_jvp_fm_none_kernel(tc, w, xd, wd, x, out):
             else:
                 nc.scalar.copy(out=dst, in_=src)
 
-        def interleave(engine, dst, src):
+        def stage_moving(raw, c, engine, under_late=False):
+            if under_late:
+                g = late.tile([P, BANK, PACK], BF16, name="under_late", align_bytes=DMA_ALIGN, offset=0)
+            else:
+                g = stage.tile([P, BANK, PACK], BF16, name="moving", align_bytes=64)
             copy(
                 engine,
-                dst.rearrange("p (c i) j -> p c j i", i=4),
-                src.rearrange("p j (c i) -> p c j i", i=4),
+                g[:].rearrange("p (c i) j -> p c j i", i=4),
+                raw[:, :, c * BANK : (c + 1) * BANK].rearrange("p j (c i) -> p c j i", i=4),
             )
-
-        def stage_moving(raw, c, engine):
-            g = stage.tile([P, T_TILE, PACK], BF16, name="g", align_bytes=64)
-            interleave(engine, g[:], raw[:, :, c * T_TILE : (c + 1) * T_TILE])
             return g
 
-        def quantise_moving(tiles, c, codes, scales, fmt):
-            cols = slice(c * T_TILE, (c + 1) * T_TILE)
+        def quantise_moving(name, staged_thirds, c):
+            codes, scales = moving[name]
+            cols = slice(c * BANK, (c + 1) * BANK)
             nc.vector.quantize_mx(
-                out=codes[:, cols].bitcast(fmt),
+                out=codes[:, cols].bitcast(fmt[name]),
                 scales=scales[:, cols],
-                in_=tiles[c][:].rearrange("p c j -> p (c j)"),
+                in_=staged_thirds[c][:].rearrange("p c j -> p (c j)"),
             )
 
-        def raw_columns(name, c0, width):
-            if name == "w":
-                return w_raw[:, :, c0 : c0 + width]
-            if c0 < EARLY:
-                return wd_early[:, :, c0 : c0 + width]
-            return wd_late[:, :, c0 - EARLY : c0 - EARLY + width]
+        def raw_tiles(name, tile, count):
+            if tile < EARLY_TILES:
+                slab = w_early[:] if name == "w" else wd_raw[:, :, :EARLY]
+                rows, first = EARLY_TILES, tile
+            else:
+                slab = w_late[:] if name == "w" else wd_raw[:, :, EARLY:]
+                rows, first = LATE_TILES, tile - EARLY_TILES
+            return slab.rearrange("p j (m r) -> p m j r", r=rows)[:, :, :, first : first + count]
 
         staged, mx = {}, {}
 
-        def stage_tile(name, tile):
-            s = stage.tile([P, P, PACK], BF16, name="s1", bufs=2, align_bytes=64)
-            interleave("v", s[:], raw_columns(name, tile * P, P))
-            staged[name, tile] = s[:].rearrange("p m j -> p (m j)")
+        def stage_tiles(name, tile, count, engine):
+            s = stage.tile([P, count, P, PACK], BF16, name="weights%d" % count, bufs=4, align_bytes=64)
+            copy(engine, s[:].rearrange("p i m j -> p m j i"), raw_tiles(name, tile, count))
+            staged[name, tile] = (s, count)
 
-        def stage_block(name, b, engine):
-            s = stage.tile([P, BLOCK, PACK], BF16, name="s2", bufs=4, align_bytes=64)
-            src = raw_columns(name, b * BLOCK, BLOCK)
-            if b in SINGLE:
-                interleave(engine, s[:], src)
-            else:
-                copy(
-                    engine,
-                    s[:].rearrange("p (i c h) j -> p c j h i", i=2, h=2),
-                    src.rearrange("p j (c h i) -> p c j h i", i=2, h=2),
-                )
-            staged[name, 2 * b] = s[:].rearrange("p m j -> p (m j)")
-
-        def quantise(name, tile, tiles):
-            codes = keep.tile([P, tiles * P], U32, name="%s_codes%d" % (name, tile), align_bytes=64)
-            scales = keep.tile([P, tiles * P], U8, name="%s_scales%d" % (name, tile), align_bytes=64)
+        def quantise(name, tile):
+            s, count = staged[name, tile]
+            codes = keep.tile([P, count * P], U32, name="%s_codes%d" % (name, tile), align_bytes=64)
+            scales = keep.tile([P, count * P], U8, name="%s_scales%d" % (name, tile), align_bytes=64)
             nc.vector.quantize_mx(
-                out=codes[:].bitcast(E4M3 if name == "w" else E5M2),
+                out=codes[:].bitcast(fmt[name]),
                 scales=scales[:],
-                in_=staged[name, tile],
+                in_=s[:].rearrange("p i m j -> p (i m j)"),
             )
-            for i in range(tiles):
+            for i in range(count):
                 mx[name, tile + i] = (codes[:, i * P : (i + 1) * P], scales[:, i * P : (i + 1) * P])
 
-        def quantise_block(name, b):
-            quantise(name, 2 * b, 2)
+        early_banks = EARLY_TILES * THIRDS
+        slabs = {}
 
-        def first_tiles(name, b):
-            stage_tile(name, 2 * b)
-            stage_tile(name, 2 * b + 1)
-            quantise(name, 2 * b, 1)
-            quantise(name, 2 * b + 1, 1)
-
-        banks, parked, results = {}, set(), {}
-
-        def result(b):
-            if b not in results:
-                results[b] = shared.tile(
-                    [P, 2, T], F32, name="result%d" % b, align_bytes=DMA_ALIGN, offset=2 * b * ROW_BYTES
+        def slab(late):
+            if late not in slabs:
+                slabs[late] = shared.tile(
+                    [P, (LATE_TILES if late else EARLY_TILES) * T],
+                    F32,
+                    name="late_result" if late else "early_result",
+                    align_bytes=DMA_ALIGN,
+                    offset=EARLY_TILES * ROW_BYTES if late else 0,
                 )
-            return results[b]
+            return slabs[late]
 
-        def target(tile, c):
-            return result(tile // 2)[:, tile % 2, c * T_TILE : (c + 1) * T_TILE]
+        def result(first, last):
+            late = first >= early_banks
+            base = early_banks if late else 0
+            return slab(late)[:, (first - base) * BANK : (last - base) * BANK]
 
-        def one_pass(name, tile, c, start, stop):
+        def store(first, last):
+            late = first >= early_banks
+            base = early_banks if late else 0
+            rows = out[EARLY:, :] if late else out[:EARLY, :]
+            flat = rows.rearrange("(m r) t -> m (r t)", m=P)
+            nc.sync.dma_start(out=flat[:, (first - base) * BANK : (last - base) * BANK], in_=result(first, last))
+
+        acc, parked = {}, set()
+
+        def one_pass(name, bank, start, stop):
+            tile, c = divmod(bank, THIRDS)
             codes, scales = mx[name, tile]
+            other_codes, other_scales = moving[partner[name]]
             if start:
-                banks[tile, c] = psum.tile([P, T_TILE], F32, name="acc")
-            cols = slice(c * T_TILE, (c + 1) * T_TILE)
+                acc[bank] = psum.tile([P, BANK], F32, name="acc")
+            cols = slice(c * BANK, (c + 1) * BANK)
             nc.tensor.matmul_mx(
-                out=banks[tile, c][:],
-                lhsT=codes.bitcast(E4M3 if name == "w" else E5M2),
+                out=acc[bank][:],
+                lhsT=codes.bitcast(fmt[name]),
                 lhsT_scale=scales,
-                rhs=(xd_codes if name == "w" else x_codes)[:, cols].bitcast(E5M2 if name == "w" else E4M3),
-                rhs_scale=(xd_scales if name == "w" else x_scales)[:, cols],
+                rhs=other_codes[:, cols].bitcast(fmt[partner[name]]),
+                rhs_scale=other_scales[:, cols],
                 start=start,
                 stop=stop,
             )
 
-        def first_name(tile):
-            return "wd" if tile * P < EARLY else "w"
+        def first_name(bank):
+            return "w" if bank < early_banks else "wd"
 
-        def second_name(tile):
-            return "w" if tile * P < EARLY else "wd"
+        def second_name(bank):
+            return "wd" if bank < early_banks else "w"
 
-        def open_banks(tile, t_tiles=range(T_TILES)):
-            for c in t_tiles:
-                if (tile, c) not in banks:
-                    one_pass(first_name(tile), tile, c, True, False)
+        def open_bank(bank):
+            one_pass(first_name(bank), bank, True, False)
 
-        def close_banks(tile):
-            for c in range(T_TILES):
-                one_pass(second_name(tile), tile, c, (tile, c) in parked, True)
+        def park(bank, engine):
+            one_pass(first_name(bank), bank, True, True)
+            copy(engine, result(bank, bank + 1), acc[bank][:])
+            parked.add(bank)
 
-        def park_pass(tile, c):
-            one_pass(first_name(tile), tile, c, True, True)
-            parked.add((tile, c))
+        runs, total = [], 0
+        for size in EARLY_STORES + LATE_STORES:
+            runs.append(range(total, total + size))
+            total = total + size
+        finished = set()
 
-        def park_copy(tile, c, engine):
-            copy(engine, target(tile, c), banks[tile, c][:])
-
-        def empty(tile, c, engine):
-            if (tile, c) in parked:
-                nc.vector.tensor_tensor(
-                    out=target(tile, c), in0=banks[tile, c][:], in1=target(tile, c), op=mybir.AluOpType.add
-                )
+        def finish(bank, engine):
+            if bank not in acc:
+                open_bank(bank)
+            one_pass(second_name(bank), bank, bank in parked, True)
+            if bank in parked:
+                target = result(bank, bank + 1)
+                nc.vector.tensor_tensor(out=target, in0=acc[bank][:], in1=target, op=mybir.AluOpType.add)
             else:
-                copy(engine, target(tile, c), banks[tile, c][:])
+                copy(engine, result(bank, bank + 1), acc[bank][:])
+            finished.add(bank)
+            for run in runs:
+                if bank in run and all(b in finished for b in run):
+                    store(run.start, run.stop)
 
-        x_staged = [stage_moving(x_raw, c, engine) for c, engine in enumerate("vsv")]
+        thirds = [stage_moving(xd_raw, c, engine) for c, engine in enumerate("vsv")]
         for c in (0, 2, 1):
-            quantise_moving(x_staged, c, x_codes, x_scales, E4M3)
-        xd_staged = [stage_moving(xd_raw, c, engine) for c, engine in enumerate("sv")]
-        stage_block("wd", 1, "s")
-        xd_staged.append(stage_moving(xd_raw, T_TILES - 1, "s"))
-        stage_block("wd", 0, "v")
-        quantise_moving(xd_staged, 0, xd_codes, xd_scales, E5M2)
-        quantise_moving(xd_staged, 1, xd_codes, xd_scales, E5M2)
-        quantise_block("wd", 1)
-        for c in range(T_TILES):
-            park_pass(3, c)
-        park_pass(2, 2)
-        open_banks(2)
-        park_copy(3, 0, "v")
-        park_copy(3, 1, "v")
-        park_copy(3, 2, "v")
-        quantise_moving(xd_staged, 2, xd_codes, xd_scales, E5M2)
-        quantise_block("wd", 0)
-        park_copy(2, 2, "v")
-        open_banks(0)
-        open_banks(1)
+            quantise_moving("xd", thirds, c)
+        for pair in (4, 2, 0):
+            stage_tiles("w", pair, 2, "s")
+        thirds = [stage_moving(x_raw, 0, "v"), stage_moving(x_raw, 1, "v", under_late=True)]
+        quantise_moving("x", thirds, 0)
+        quantise("w", 4)
+        thirds.append(stage_moving(x_raw, 2, "v"))
+        quantise("w", 2)
+        quantise("w", 0)
+        quantise_moving("x", thirds, 1)
+        w_late = late.tile([P, PACK, N - EARLY], F32, name="w_late", align_bytes=DMA_ALIGN, offset=0)
+        nc.sync.dma_start(out=w_late[:], in_=view(w)[:, :, EARLY:])
+        quantise_moving("x", thirds, 2)
+        for bank in range(15, 7, -1):
+            park(bank, "v" if bank in (8, 10) else "s")
+        for bank in range(8):
+            open_bank(bank)
 
-        first_tiles("w", 0)
-        stage_block("w", 3, "s")
-        stage_block("w", 1, "v")
-        quantise_block("w", 3)
-        quantise_block("w", 1)
-
-        def run_ahead():
-            for c in range(T_TILES):
-                park_pass(7, c)
-            for c in range(T_TILES):
-                park_copy(7, c, "s")
-            open_banks(4)
-            open_banks(5)
-            open_banks(6, range(2))
-
-        after = {
-            0: [lambda: stage_block("w", 2, "v"), lambda: quantise_block("w", 2)],
-            3: [
-                run_ahead,
-                lambda: first_tiles("wd", 2),
-                lambda: stage_block("wd", 3, "v"),
-                lambda: stage_block("w", 4, "s"),
-            ],
-            4: [lambda: quantise_block("wd", 3), lambda: stage_block("wd", 4, "v"), lambda: quantise_block("w", 4)],
-            5: [lambda: stage_block("w", 5, "v"), lambda: quantise_block("wd", 4)],
-        }
-        for b in range(5, BLOCKS):
-            after[2 * b - 3] = [lambda b=b: quantise_block("w", b), lambda b=b: stage_block("wd", b, "v")]
-            after[2 * b - 2] = [lambda b=b: quantise_block("wd", b)]
-            if b + 1 < BLOCKS:
-                after[2 * b - 2].append(lambda b=b: stage_block("w", b + 1, "v"))
-        scalar_alone = (1, 5, 6)
-
-        for b in range(BLOCKS):
-            rows = out[b * BLOCK : (b + 1) * BLOCK, :]
-            for i in range(2):
-                tile = 2 * b + i
-                open_banks(tile)
-                close_banks(tile)
-                for c in range(T_TILES):
-                    empty(tile, c, "v" if c == T_TILES - 1 and tile not in scalar_alone else "s")
-                for step in after.get(tile, []):
-                    step()
-                if b in SINGLE:
-                    nc.sync.dma_start(out=rows[i * P : (i + 1) * P, :], in_=result(b)[:, i, :])
-            if b not in SINGLE:
-                nc.sync.dma_start(out=rows.rearrange("(m i) t -> m i t", i=2), in_=result(b)[:])
+        stage_tiles("wd", 0, 1, "v")
+        stage_tiles("wd", 1, 1, "v")
+        stage_tiles("wd", 2, 2, "s")
+        quantise("wd", 0)
+        quantise("wd", 1)
+        stage_tiles("wd", 4, 2, "v")
+        quantise("wd", 2)
+        for bank, engine in enumerate("svsvssss"):
+            finish(bank, engine)
+            if bank == 3:
+                quantise("wd", 4)
+                stage_tiles("wd", 6, 2, "v")
+        finish(8, "v")
+        quantise("wd", 6)
+        for bank in range(9, 12):
+            finish(bank, "v")
+        finish(16, "s")
+        finish(12, "v")
+        stage_tiles("w", 6, 2, "s")
+        open_bank(17)
+        open_bank(18)
+        open_bank(19)
+        quantise("w", 6)
+        finish(13, "v")
+        stage_tiles("wd", 8, 2, "s")
+        open_bank(20)
+        open_bank(21)
+        finish(14, "v")
+        finish(17, "s")
+        finish(15, "v")
+        quantise("wd", 8)
+        stage_tiles("w", 8, 2, "v")
+        quantise("w", 8)
+        for pair in range(6, TILES, 2):
+            first, ahead = pair * THIRDS, pair + 2
+            if pair > 6:
+                for bank in range(first, first + (THIRDS if pair < 12 else 2)):
+                    open_bank(bank)
+            for i, engine in enumerate({6: "sssvss", 8: "svssss"}.get(pair, "vssvss")):
+                finish(first + i, engine)
+                if pair == 6 and i == 3:
+                    stage_tiles("wd", 10, 2, "v")
+                if pair > 6 and ahead < TILES:
+                    if i == (1 if pair == 8 else 0):
+                        quantise("wd", ahead)
+                        stage_tiles("w", ahead, 2, "v")
+                    if i == 3:
+                        quantise("w", ahead)
+                        if ahead + 2 < TILES:
+                            stage_tiles("wd", ahead + 2, 2, "v")

@@ -17,23 +17,22 @@ PACK = 4
 BANK = 512
 THIRDS = T // BANK
 TILES = N // P
-EARLY_TILES = 6
+EARLY_TILES = 4
 LATE_TILES = TILES - EARLY_TILES
 EARLY = EARLY_TILES * P
 DMA_ALIGN = 256
 ROW_BYTES = 4 * T
-EARLY_STORES = (5, 6, 7)
-LATE_STORES = (10, 10, 10)
+EARLY_STORES = (4, 8)
+LATE_STORES = (7, 8, 7, 7, 7)
 
 
 def tile_mix_jvp_fm_none_kernel(tc, w, xd, wd, x, out):
     nc = tc.nc
     with ExitStack() as ctx:
         shared = ctx.enter_context(tc.tile_pool(name="shared", bufs=1))
-        late = ctx.enter_context(tc.tile_pool(name="late", bufs=1))
         keep = ctx.enter_context(tc.tile_pool(name="keep", bufs=1))
         stage = ctx.enter_context(tc.tile_pool(name="stage", bufs=3))
-        psum = ctx.enter_context(tc.psum_pool(name="psum", bufs=8))
+        psum = ctx.enter_context(tc.psum_pool(name="psum", bufs=1))
         ctx.enter_context(tc.manual_schedule())
 
         def view(a):
@@ -47,6 +46,8 @@ def tile_mix_jvp_fm_none_kernel(tc, w, xd, wd, x, out):
         nc.gpsimd.dma_start(out=x_raw[:], in_=view(x))
         wd_raw = keep.tile([P, PACK, N], F32, name="wd_raw", align_bytes=DMA_ALIGN)
         nc.gpsimd.dma_start(out=wd_raw[:], in_=view(wd))
+        w_late = keep.tile([P, PACK, N - EARLY], F32, name="w_late", align_bytes=DMA_ALIGN)
+        nc.gpsimd.dma_start(out=w_late[:], in_=view(w)[:, :, EARLY:])
 
         moving = {}
         for name in ("xd", "x"):
@@ -62,11 +63,8 @@ def tile_mix_jvp_fm_none_kernel(tc, w, xd, wd, x, out):
             else:
                 nc.scalar.copy(out=dst, in_=src)
 
-        def stage_moving(raw, c, engine, under_late=False):
-            if under_late:
-                g = late.tile([P, BANK, PACK], BF16, name="under_late", align_bytes=DMA_ALIGN, offset=0)
-            else:
-                g = stage.tile([P, BANK, PACK], BF16, name="moving", align_bytes=64)
+        def stage_moving(raw, c, engine):
+            g = stage.tile([P, BANK, PACK], BF16, name="moving", align_bytes=64)
             copy(
                 engine,
                 g[:].rearrange("p (c i) j -> p c j i", i=4),
@@ -94,24 +92,26 @@ def tile_mix_jvp_fm_none_kernel(tc, w, xd, wd, x, out):
 
         staged, mx = {}, {}
 
-        def stage_tiles(name, tile, count, engine):
-            s = stage.tile([P, count, P, PACK], BF16, name="weights%d" % count, bufs=4, align_bytes=64)
-            copy(engine, s[:].rearrange("p i m j -> p m j i"), raw_tiles(name, tile, count))
-            staged[name, tile] = (s, count)
+        def stage_pair(name, tile, engine):
+            s = stage.tile([P, 2, P, PACK], BF16, name="weights", bufs=4, align_bytes=64)
+            copy(engine, s[:].rearrange("p i m j -> p m j i"), raw_tiles(name, tile, 2))
+            staged[name, tile] = s[:].rearrange("p i m j -> p (i m j)")
+            staged[name, tile + 1] = staged[name, tile][:, P * PACK :]
 
-        def quantise(name, tile):
-            s, count = staged[name, tile]
+        def quantise(name, tile, count=2):
             codes = keep.tile([P, count * P], U32, name="%s_codes%d" % (name, tile), align_bytes=64)
             scales = keep.tile([P, count * P], U8, name="%s_scales%d" % (name, tile), align_bytes=64)
             nc.vector.quantize_mx(
                 out=codes[:].bitcast(fmt[name]),
                 scales=scales[:],
-                in_=s[:].rearrange("p i m j -> p (i m j)"),
+                in_=staged[name, tile][:, : count * P * PACK],
             )
             for i in range(count):
                 mx[name, tile + i] = (codes[:, i * P : (i + 1) * P], scales[:, i * P : (i + 1) * P])
 
         early_banks = EARLY_TILES * THIRDS
+        held = range(8)
+        parks = range(8, early_banks)
         slabs = {}
 
         def slab(late):
@@ -135,16 +135,20 @@ def tile_mix_jvp_fm_none_kernel(tc, w, xd, wd, x, out):
             base = early_banks if late else 0
             rows = out[EARLY:, :] if late else out[:EARLY, :]
             flat = rows.rearrange("(m r) t -> m (r t)", m=P)
-            nc.sync.dma_start(out=flat[:, (first - base) * BANK : (last - base) * BANK], in_=result(first, last))
+            queue = nc.gpsimd if first == 0 else nc.sync
+            queue.dma_start(out=flat[:, (first - base) * BANK : (last - base) * BANK], in_=result(first, last))
 
-        acc, parked = {}, set()
+        acc, parked, slot = {}, set(), {}
+        free = list(range(8))
 
         def one_pass(name, bank, start, stop):
             tile, c = divmod(bank, THIRDS)
             codes, scales = mx[name, tile]
             other_codes, other_scales = moving[partner[name]]
             if start:
-                acc[bank] = psum.tile([P, BANK], F32, name="acc")
+                slot[bank] = free[0]
+                free.remove(slot[bank])
+                acc[bank] = psum.tile([P, BANK], F32, name="acc%d" % slot[bank])
             cols = slice(c * BANK, (c + 1) * BANK)
             nc.tensor.matmul_mx(
                 out=acc[bank][:],
@@ -169,6 +173,7 @@ def tile_mix_jvp_fm_none_kernel(tc, w, xd, wd, x, out):
             one_pass(first_name(bank), bank, True, True)
             copy(engine, result(bank, bank + 1), acc[bank][:])
             parked.add(bank)
+            free.append(slot[bank])
 
         runs, total = [], 0
         for size in EARLY_STORES + LATE_STORES:
@@ -176,10 +181,11 @@ def tile_mix_jvp_fm_none_kernel(tc, w, xd, wd, x, out):
             total = total + size
         finished = set()
 
-        def finish(bank, engine):
-            if bank not in acc:
-                open_bank(bank)
+        def close_bank(bank):
             one_pass(second_name(bank), bank, bank in parked, True)
+
+        def empty(bank, engine):
+            free.append(slot[bank])
             if bank in parked:
                 target = result(bank, bank + 1)
                 nc.vector.tensor_tensor(out=target, in0=acc[bank][:], in1=target, op=mybir.AluOpType.add)
@@ -193,70 +199,82 @@ def tile_mix_jvp_fm_none_kernel(tc, w, xd, wd, x, out):
         thirds = [stage_moving(xd_raw, c, engine) for c, engine in enumerate("vsv")]
         for c in (0, 2, 1):
             quantise_moving("xd", thirds, c)
-        for pair in (4, 2, 0):
-            stage_tiles("w", pair, 2, "s")
-        thirds = [stage_moving(x_raw, 0, "v"), stage_moving(x_raw, 1, "v", under_late=True)]
+        for pair in (2, 0):
+            stage_pair("w", pair, "s")
+        thirds = [stage_moving(x_raw, c, "v") for c in range(THIRDS)]
         quantise_moving("x", thirds, 0)
-        quantise("w", 4)
-        thirds.append(stage_moving(x_raw, 2, "v"))
         quantise("w", 2)
         quantise("w", 0)
         quantise_moving("x", thirds, 1)
-        w_late = late.tile([P, PACK, N - EARLY], F32, name="w_late", align_bytes=DMA_ALIGN, offset=0)
-        nc.sync.dma_start(out=w_late[:], in_=view(w)[:, :, EARLY:])
         quantise_moving("x", thirds, 2)
-        for bank in range(15, 7, -1):
-            park(bank, "v" if bank in (8, 10) else "s")
-        for bank in range(8):
+        for bank in reversed(parks):
+            park(bank, "s")
+        for bank in held:
             open_bank(bank)
 
-        stage_tiles("wd", 0, 1, "v")
-        stage_tiles("wd", 1, 1, "v")
-        stage_tiles("wd", 2, 2, "s")
-        quantise("wd", 0)
-        quantise("wd", 1)
-        stage_tiles("wd", 4, 2, "v")
+        stage_pair("wd", 0, "v")
+        stage_pair("wd", 2, "s")
+        quantise("wd", 0, 1)
+        quantise("wd", 1, 1)
+        stage_pair("wd", 6, "v")
         quantise("wd", 2)
-        for bank, engine in enumerate("svsvssss"):
-            finish(bank, engine)
+        for bank, engine in zip(held, "svsvsvss"):
+            close_bank(bank)
+            empty(bank, engine)
             if bank == 3:
-                quantise("wd", 4)
-                stage_tiles("wd", 6, 2, "v")
-        finish(8, "v")
-        quantise("wd", 6)
-        for bank in range(9, 12):
-            finish(bank, "v")
-        finish(16, "s")
-        finish(12, "v")
-        stage_tiles("w", 6, 2, "s")
-        open_bank(17)
+                quantise("wd", 6)
+            if bank == 4:
+                stage_pair("wd", 4, "s")
+        for bank in parks:
+            close_bank(bank)
+        empty(8, "v")
+        park(23, "s")
+        park(22, "s")
+        empty(9, "v")
+        quantise("wd", 4)
         open_bank(18)
         open_bank(19)
+        open_bank(12)
+        empty(10, "v")
+        open_bank(13)
+        open_bank(14)
+        empty(11, "v")
+        open_bank(15)
+        open_bank(16)
+        open_bank(17)
+
+        stage_pair("w", 4, "v")
+        stage_pair("w", 6, "s")
+        quantise("w", 4, 1)
+        quantise("w", 5, 1)
+        stage_pair("wd", 8, "v")
         quantise("w", 6)
-        finish(13, "v")
-        stage_tiles("wd", 8, 2, "s")
+        for bank, engine in zip(range(12, 20), "svsvsvss"):
+            close_bank(bank)
+            empty(bank, engine)
+            if bank == 13:
+                quantise("wd", 8)
+            if bank == 17:
+                stage_pair("w", 8, "v")
         open_bank(20)
         open_bank(21)
-        finish(14, "v")
-        finish(17, "s")
-        finish(15, "v")
-        quantise("wd", 8)
-        stage_tiles("w", 8, 2, "v")
-        quantise("w", 8)
-        for pair in range(6, TILES, 2):
-            first, ahead = pair * THIRDS, pair + 2
-            if pair > 6:
-                for bank in range(first, first + (THIRDS if pair < 12 else 2)):
-                    open_bank(bank)
-            for i, engine in enumerate({6: "sssvss", 8: "svssss"}.get(pair, "vssvss")):
-                finish(first + i, engine)
-                if pair == 6 and i == 3:
-                    stage_tiles("wd", 10, 2, "v")
-                if pair > 6 and ahead < TILES:
-                    if i == (1 if pair == 8 else 0):
-                        quantise("wd", ahead)
-                        stage_tiles("w", ahead, 2, "v")
-                    if i == 3:
-                        quantise("w", ahead)
-                        if ahead + 2 < TILES:
-                            stage_tiles("wd", ahead + 2, 2, "v")
+        for bank, engine in zip(range(20, 24), "ssvv"):
+            close_bank(bank)
+            empty(bank, engine)
+            if bank == 22:
+                quantise("w", 8)
+        stage_pair("wd", 10, "v")
+        for tile in range(8, TILES):
+            first = tile * THIRDS
+            for bank in range(first, first + THIRDS):
+                open_bank(bank)
+            for bank, engine in zip(range(first, first + THIRDS), "vss" if tile % 2 == 1 and tile + 1 < TILES else "svs"):
+                close_bank(bank)
+                empty(bank, engine)
+            if tile % 2 == 1 and tile + 1 < TILES:
+                quantise("w", tile + 1)
+            if tile % 2 == 0 and tile + 2 < TILES:
+                quantise("wd", tile + 2)
+                stage_pair("w", tile + 2, "v")
+            if tile % 2 == 1 and tile + 3 < TILES:
+                stage_pair("wd", tile + 3, "v")

@@ -41,13 +41,13 @@ def tile_mix_jvp_fm_none_kernel(tc, w, xd, wd, x, out):
         xd_raw = shared.tile([P, PACK, T], F32, name="xd_raw", align_bytes=DMA_ALIGN, offset=0)
         nc.sync.dma_start(out=xd_raw[:], in_=view(xd))
         w_early = keep.tile([P, PACK, EARLY], F32, name="w_early", align_bytes=DMA_ALIGN)
-        nc.gpsimd.dma_start(out=w_early[:], in_=view(w)[:, :, :EARLY])
+        nc.sync.dma_start(out=w_early[:], in_=view(w)[:, :, :EARLY])
         x_raw = shared.tile([P, PACK, T], F32, name="x_raw", align_bytes=DMA_ALIGN, offset=EARLY_TILES * ROW_BYTES)
-        nc.gpsimd.dma_start(out=x_raw[:], in_=view(x))
+        nc.sync.dma_start(out=x_raw[:], in_=view(x))
         wd_raw = keep.tile([P, PACK, N], F32, name="wd_raw", align_bytes=DMA_ALIGN)
-        nc.gpsimd.dma_start(out=wd_raw[:], in_=view(wd))
+        nc.sync.dma_start(out=wd_raw[:], in_=view(wd))
         w_late = keep.tile([P, PACK, N - EARLY], F32, name="w_late", align_bytes=DMA_ALIGN)
-        nc.gpsimd.dma_start(out=w_late[:], in_=view(w)[:, :, EARLY:])
+        nc.sync.dma_start(out=w_late[:], in_=view(w)[:, :, EARLY:])
 
         moving = {}
         for name in ("xd", "x"):
@@ -135,8 +135,7 @@ def tile_mix_jvp_fm_none_kernel(tc, w, xd, wd, x, out):
             base = early_banks if late else 0
             rows = out[EARLY:, :] if late else out[:EARLY, :]
             flat = rows.rearrange("(m r) t -> m (r t)", m=P)
-            queue = nc.gpsimd if first == 0 else nc.sync
-            queue.dma_start(out=flat[:, (first - base) * BANK : (last - base) * BANK], in_=result(first, last))
+            nc.sync.dma_start(out=flat[:, (first - base) * BANK : (last - base) * BANK], in_=result(first, last))
 
         acc, parked, slot = {}, set(), {}
         free = list(range(8))

@@ -22,14 +22,16 @@ LATE_TILES = TILES - EARLY_TILES
 EARLY = EARLY_TILES * P
 DMA_ALIGN = 256
 ROW_BYTES = 4 * T
-EARLY_STORES = (4, 8)
-LATE_STORES = (7, 8, 7, 7, 7)
+EARLY_STORES = (6, 6)
+LATE_STORES = (8, 10, 9, 9)
+VECTOR_ROWS = 76
 
 
 def tile_mix_jvp_fm_none_kernel(tc, w, xd, wd, x, out):
     nc = tc.nc
     with ExitStack() as ctx:
         shared = ctx.enter_context(tc.tile_pool(name="shared", bufs=1))
+        late = ctx.enter_context(tc.tile_pool(name="late", bufs=1))
         keep = ctx.enter_context(tc.tile_pool(name="keep", bufs=1))
         stage = ctx.enter_context(tc.tile_pool(name="stage", bufs=3))
         psum = ctx.enter_context(tc.psum_pool(name="psum", bufs=1))
@@ -38,16 +40,14 @@ def tile_mix_jvp_fm_none_kernel(tc, w, xd, wd, x, out):
         def view(a):
             return a.rearrange("(p j) c -> p j c", j=PACK)
 
-        xd_raw = shared.tile([P, PACK, T], F32, name="xd_raw", align_bytes=DMA_ALIGN, offset=0)
-        nc.sync.dma_start(out=xd_raw[:], in_=view(xd))
         w_early = keep.tile([P, PACK, EARLY], F32, name="w_early", align_bytes=DMA_ALIGN)
         nc.sync.dma_start(out=w_early[:], in_=view(w)[:, :, :EARLY])
+        xd_raw = shared.tile([P, PACK, T], F32, name="xd_raw", align_bytes=DMA_ALIGN, offset=0)
+        nc.gpsimd.dma_start(out=xd_raw[:], in_=view(xd))
         x_raw = shared.tile([P, PACK, T], F32, name="x_raw", align_bytes=DMA_ALIGN, offset=EARLY_TILES * ROW_BYTES)
-        nc.sync.dma_start(out=x_raw[:], in_=view(x))
+        nc.gpsimd.dma_start(out=x_raw[:], in_=view(x))
         wd_raw = keep.tile([P, PACK, N], F32, name="wd_raw", align_bytes=DMA_ALIGN)
-        nc.sync.dma_start(out=wd_raw[:], in_=view(wd))
-        w_late = keep.tile([P, PACK, N - EARLY], F32, name="w_late", align_bytes=DMA_ALIGN)
-        nc.sync.dma_start(out=w_late[:], in_=view(w)[:, :, EARLY:])
+        nc.gpsimd.dma_start(out=wd_raw[:], in_=view(wd))
 
         moving = {}
         for name in ("xd", "x"):
@@ -63,8 +63,11 @@ def tile_mix_jvp_fm_none_kernel(tc, w, xd, wd, x, out):
             else:
                 nc.scalar.copy(out=dst, in_=src)
 
-        def stage_moving(raw, c, engine):
-            g = stage.tile([P, BANK, PACK], BF16, name="moving", align_bytes=64)
+        def stage_moving(raw, c, engine, under_late=False):
+            if under_late:
+                g = late.tile([P, BANK, PACK], BF16, name="under_late", align_bytes=DMA_ALIGN, offset=0)
+            else:
+                g = stage.tile([P, BANK, PACK], BF16, name="moving", align_bytes=64)
             copy(
                 engine,
                 g[:].rearrange("p (c i) j -> p c j i", i=4),
@@ -94,7 +97,12 @@ def tile_mix_jvp_fm_none_kernel(tc, w, xd, wd, x, out):
 
         def stage_pair(name, tile, engine):
             s = stage.tile([P, 2, P, PACK], BF16, name="weights", bufs=4, align_bytes=64)
-            copy(engine, s[:].rearrange("p i m j -> p m j i"), raw_tiles(name, tile, 2))
+            dst, src = s[:].rearrange("p i m j -> p m j i"), raw_tiles(name, tile, 2)
+            if engine == "both":
+                copy("v", dst[:, :VECTOR_ROWS], src[:, :VECTOR_ROWS])
+                copy("s", dst[:, VECTOR_ROWS:], src[:, VECTOR_ROWS:])
+            else:
+                copy(engine, dst, src)
             staged[name, tile] = s[:].rearrange("p i m j -> p (i m j)")
             staged[name, tile + 1] = staged[name, tile][:, P * PACK :]
 
@@ -140,17 +148,19 @@ def tile_mix_jvp_fm_none_kernel(tc, w, xd, wd, x, out):
         acc, parked, slot = {}, set(), {}
         free = list(range(8))
 
-        def one_pass(name, bank, start, stop):
+        def one_pass(name, bank, start, stop, half=None):
             tile, c = divmod(bank, THIRDS)
             codes, scales = mx[name, tile]
             other_codes, other_scales = moving[partner[name]]
+            key = bank if half is None else (bank, half)
+            width = BANK if half is None else BANK // 2
             if start:
-                slot[bank] = free[0]
-                free.remove(slot[bank])
-                acc[bank] = psum.tile([P, BANK], F32, name="acc%d" % slot[bank])
-            cols = slice(c * BANK, (c + 1) * BANK)
+                slot[key] = free[0]
+                free.remove(slot[key])
+                acc[key] = psum.tile([P, width], F32, name="acc%d" % slot[key])
+            cols = slice(c * BANK + (half or 0) * width, c * BANK + ((half or 0) + 1) * width)
             nc.tensor.matmul_mx(
-                out=acc[bank][:],
+                out=acc[key][:],
                 lhsT=codes.bitcast(fmt[name]),
                 lhsT_scale=scales,
                 rhs=other_codes[:, cols].bitcast(fmt[partner[name]]),
@@ -190,6 +200,9 @@ def tile_mix_jvp_fm_none_kernel(tc, w, xd, wd, x, out):
                 nc.vector.tensor_tensor(out=target, in0=acc[bank][:], in1=target, op=mybir.AluOpType.add)
             else:
                 copy(engine, result(bank, bank + 1), acc[bank][:])
+            done(bank)
+
+        def done(bank):
             finished.add(bank)
             for run in runs:
                 if bank in run and all(b in finished for b in run):
@@ -200,80 +213,104 @@ def tile_mix_jvp_fm_none_kernel(tc, w, xd, wd, x, out):
             quantise_moving("xd", thirds, c)
         for pair in (2, 0):
             stage_pair("w", pair, "s")
-        thirds = [stage_moving(x_raw, c, "v") for c in range(THIRDS)]
+        thirds = [stage_moving(x_raw, c, "v", under_late=c == 1) for c in range(THIRDS)]
         quantise_moving("x", thirds, 0)
         quantise("w", 2)
         quantise("w", 0)
         quantise_moving("x", thirds, 1)
+        w_late = late.tile([P, PACK, N - EARLY], F32, name="w_late", align_bytes=DMA_ALIGN, offset=0)
+        nc.sync.dma_start(out=w_late[:], in_=view(w)[:, :, EARLY:])
         quantise_moving("x", thirds, 2)
         for bank in reversed(parks):
             park(bank, "s")
         for bank in held:
             open_bank(bank)
 
-        stage_pair("wd", 0, "v")
+        stage_pair("wd", 0, "both")
         stage_pair("wd", 2, "s")
         quantise("wd", 0, 1)
         quantise("wd", 1, 1)
         stage_pair("wd", 6, "v")
-        quantise("wd", 2)
-        for bank, engine in zip(held, "svsvsvss"):
+        for bank, engine in zip(held, "vsvsssss"):
             close_bank(bank)
-            empty(bank, engine)
-            if bank == 3:
+            if bank < 6:
+                empty(bank, engine)
+            if bank == 0:
+                quantise("wd", 2)
                 quantise("wd", 6)
-            if bank == 4:
-                stage_pair("wd", 4, "s")
+            if bank == 2:
+                stage_pair("wd", 4, "v")
         for bank in parks:
             close_bank(bank)
         empty(8, "v")
-        park(23, "s")
-        park(22, "s")
-        empty(9, "v")
+        empty(6, "s")
+        empty(7, "s")
         quantise("wd", 4)
-        open_bank(18)
-        open_bank(19)
-        open_bank(12)
+        empty(9, "v")
+        park(23, "s")
         empty(10, "v")
-        open_bank(13)
-        open_bank(14)
+        park(22, "s")
         empty(11, "v")
-        open_bank(15)
-        open_bank(16)
-        open_bank(17)
+        park(21, "s")
+        for bank in (18, 19, 12, 13, 14, 15, 16, 17):
+            open_bank(bank)
 
-        stage_pair("w", 4, "v")
+        stage_pair("w", 4, "both")
         stage_pair("w", 6, "s")
         quantise("w", 4, 1)
         quantise("w", 5, 1)
         stage_pair("wd", 8, "v")
-        quantise("w", 6)
-        for bank, engine in zip(range(12, 20), "svsvsvss"):
+        for bank, engine in zip(range(12, 20), "vsvsvsvs"):
             close_bank(bank)
             empty(bank, engine)
-            if bank == 13:
-                quantise("wd", 8)
-            if bank == 17:
-                stage_pair("w", 8, "v")
+            if bank == 12:
+                quantise("w", 6)
+        quantise("wd", 8)
+        stage_pair("w", 8, "v")
         open_bank(20)
-        open_bank(21)
-        for bank, engine in zip(range(20, 24), "ssvv"):
+        for bank, engine in zip(range(20, 24), "svvv"):
             close_bank(bank)
             empty(bank, engine)
-            if bank == 22:
+            if bank == 21:
                 quantise("w", 8)
-        stage_pair("wd", 10, "v")
-        for tile in range(8, TILES):
-            first = tile * THIRDS
-            for bank in range(first, first + THIRDS):
-                open_bank(bank)
-            for bank, engine in zip(range(first, first + THIRDS), "vss" if tile % 2 == 1 and tile + 1 < TILES else "svs"):
-                close_bank(bank)
-                empty(bank, engine)
-            if tile % 2 == 1 and tile + 1 < TILES:
-                quantise("w", tile + 1)
-            if tile % 2 == 0 and tile + 2 < TILES:
-                quantise("wd", tile + 2)
-                stage_pair("w", tile + 2, "v")
-            if tile % 2 == 1 and tile + 3 < TILES:
-                stage_pair("wd", tile + 3, "v")
+        stage_pair("wd", 10, "s")
+        quantise("wd", 10)
+
+        def run_of(first, engines):
+            banks = range(first, first + len(engines))
+            for bank, engine in zip(banks, engines):
+                if engine == "h":
+                    one_pass("wd", bank, True, False, 0)
+                    one_pass("wd", bank, True, False, 1)
+                else:
+                    open_bank(bank)
+            for bank, engine in zip(banks, engines):
+                if engine == "h":
+                    for half, engine_of_half in enumerate("sv"):
+                        one_pass("w", bank, False, True, half)
+                        free.append(slot[bank, half])
+                        cols = slice(half * BANK // 2, (half + 1) * BANK // 2)
+                        copy(engine_of_half, result(bank, bank + 1)[:, cols], acc[bank, half][:])
+                    done(bank)
+                else:
+                    close_bank(bank)
+                    empty(bank, engine)
+
+        run_of(24, "ssvsv")
+        run_of(29, "h")
+        stage_pair("w", 10, "both")
+        stage_pair("wd", 12, "s")
+        quantise("w", 10)
+        stage_pair("w", 12, "v")
+        quantise("wd", 12)
+        quantise("w", 12)
+        run_of(30, "svsvsv")
+        stage_pair("wd", 14, "both")
+        run_of(36, "sv")
+        run_of(38, "h")
+        quantise("wd", 14)
+        stage_pair("w", 14, "v")
+        run_of(39, "ssv")
+        quantise("w", 14)
+        run_of(42, "vsvsv")
+        run_of(47, "h")

@@ -22,8 +22,8 @@ LATE_TILES = TILES - EARLY_TILES
 EARLY = EARLY_TILES * P
 DMA_ALIGN = 256
 ROW_BYTES = 4 * T
-EARLY_STORES = (6, 6)
-LATE_STORES = (8, 10, 9, 9)
+EARLY_STORES = (5, 7)
+LATE_STORES = (6, 6, 6, 6, 6, 6)
 VECTOR_ROWS = 76
 
 
@@ -31,7 +31,6 @@ def tile_mix_jvp_fm_none_kernel(tc, w, xd, wd, x, out):
     nc = tc.nc
     with ExitStack() as ctx:
         shared = ctx.enter_context(tc.tile_pool(name="shared", bufs=1))
-        late = ctx.enter_context(tc.tile_pool(name="late", bufs=1))
         keep = ctx.enter_context(tc.tile_pool(name="keep", bufs=1))
         stage = ctx.enter_context(tc.tile_pool(name="stage", bufs=3))
         psum = ctx.enter_context(tc.psum_pool(name="psum", bufs=1))
@@ -40,14 +39,16 @@ def tile_mix_jvp_fm_none_kernel(tc, w, xd, wd, x, out):
         def view(a):
             return a.rearrange("(p j) c -> p j c", j=PACK)
 
-        w_early = keep.tile([P, PACK, EARLY], F32, name="w_early", align_bytes=DMA_ALIGN)
-        nc.sync.dma_start(out=w_early[:], in_=view(w)[:, :, :EARLY])
         xd_raw = shared.tile([P, PACK, T], F32, name="xd_raw", align_bytes=DMA_ALIGN, offset=0)
-        nc.gpsimd.dma_start(out=xd_raw[:], in_=view(xd))
+        nc.sync.dma_start(out=xd_raw[:], in_=view(xd))
+        w_early = keep.tile([P, PACK, EARLY], F32, name="w_early", align_bytes=DMA_ALIGN)
+        nc.scalar.dma_start(out=w_early[:], in_=view(w)[:, :, :EARLY])
         x_raw = shared.tile([P, PACK, T], F32, name="x_raw", align_bytes=DMA_ALIGN, offset=EARLY_TILES * ROW_BYTES)
-        nc.gpsimd.dma_start(out=x_raw[:], in_=view(x))
+        nc.sync.dma_start(out=x_raw[:], in_=view(x))
         wd_raw = keep.tile([P, PACK, N], F32, name="wd_raw", align_bytes=DMA_ALIGN)
-        nc.gpsimd.dma_start(out=wd_raw[:], in_=view(wd))
+        nc.sync.dma_start(out=wd_raw[:], in_=view(wd))
+        w_late = keep.tile([P, PACK, N - EARLY], F32, name="w_late", align_bytes=DMA_ALIGN)
+        nc.sync.dma_start(out=w_late[:], in_=view(w)[:, :, EARLY:])
 
         moving = {}
         for name in ("xd", "x"):
@@ -63,11 +64,8 @@ def tile_mix_jvp_fm_none_kernel(tc, w, xd, wd, x, out):
             else:
                 nc.scalar.copy(out=dst, in_=src)
 
-        def stage_moving(raw, c, engine, under_late=False):
-            if under_late:
-                g = late.tile([P, BANK, PACK], BF16, name="under_late", align_bytes=DMA_ALIGN, offset=0)
-            else:
-                g = stage.tile([P, BANK, PACK], BF16, name="moving", align_bytes=64)
+        def stage_moving(raw, c, engine):
+            g = stage.tile([P, BANK, PACK], BF16, name="moving", align_bytes=64)
             copy(
                 engine,
                 g[:].rearrange("p (c i) j -> p c j i", i=4),
@@ -148,19 +146,17 @@ def tile_mix_jvp_fm_none_kernel(tc, w, xd, wd, x, out):
         acc, parked, slot = {}, set(), {}
         free = list(range(8))
 
-        def one_pass(name, bank, start, stop, half=None):
+        def one_pass(name, bank, start, stop):
             tile, c = divmod(bank, THIRDS)
             codes, scales = mx[name, tile]
             other_codes, other_scales = moving[partner[name]]
-            key = bank if half is None else (bank, half)
-            width = BANK if half is None else BANK // 2
             if start:
-                slot[key] = free[0]
-                free.remove(slot[key])
-                acc[key] = psum.tile([P, width], F32, name="acc%d" % slot[key])
-            cols = slice(c * BANK + (half or 0) * width, c * BANK + ((half or 0) + 1) * width)
+                slot[bank] = free[0]
+                free.remove(slot[bank])
+                acc[bank] = psum.tile([P, BANK], F32, name="acc%d" % slot[bank])
+            cols = slice(c * BANK, (c + 1) * BANK)
             nc.tensor.matmul_mx(
-                out=acc[key][:],
+                out=acc[bank][:],
                 lhsT=codes.bitcast(fmt[name]),
                 lhsT_scale=scales,
                 rhs=other_codes[:, cols].bitcast(fmt[partner[name]]),
@@ -200,9 +196,6 @@ def tile_mix_jvp_fm_none_kernel(tc, w, xd, wd, x, out):
                 nc.vector.tensor_tensor(out=target, in0=acc[bank][:], in1=target, op=mybir.AluOpType.add)
             else:
                 copy(engine, result(bank, bank + 1), acc[bank][:])
-            done(bank)
-
-        def done(bank):
             finished.add(bank)
             for run in runs:
                 if bank in run and all(b in finished for b in run):
@@ -213,13 +206,11 @@ def tile_mix_jvp_fm_none_kernel(tc, w, xd, wd, x, out):
             quantise_moving("xd", thirds, c)
         for pair in (2, 0):
             stage_pair("w", pair, "s")
-        thirds = [stage_moving(x_raw, c, "v", under_late=c == 1) for c in range(THIRDS)]
+        thirds = [stage_moving(x_raw, c, "v") for c in range(THIRDS)]
         quantise_moving("x", thirds, 0)
         quantise("w", 2)
         quantise("w", 0)
         quantise_moving("x", thirds, 1)
-        w_late = late.tile([P, PACK, N - EARLY], F32, name="w_late", align_bytes=DMA_ALIGN, offset=0)
-        nc.sync.dma_start(out=w_late[:], in_=view(w)[:, :, EARLY:])
         quantise_moving("x", thirds, 2)
         for bank in reversed(parks):
             park(bank, "s")
@@ -274,43 +265,18 @@ def tile_mix_jvp_fm_none_kernel(tc, w, xd, wd, x, out):
             if bank == 21:
                 quantise("w", 8)
         stage_pair("wd", 10, "s")
+        stage_pair("w", 10, "s")
         quantise("wd", 10)
-
-        def run_of(first, engines):
-            banks = range(first, first + len(engines))
-            for bank, engine in zip(banks, engines):
-                if engine == "h":
-                    one_pass("wd", bank, True, False, 0)
-                    one_pass("wd", bank, True, False, 1)
-                else:
-                    open_bank(bank)
-            for bank, engine in zip(banks, engines):
-                if engine == "h":
-                    for half, engine_of_half in enumerate("sv"):
-                        one_pass("w", bank, False, True, half)
-                        free.append(slot[bank, half])
-                        cols = slice(half * BANK // 2, (half + 1) * BANK // 2)
-                        copy(engine_of_half, result(bank, bank + 1)[:, cols], acc[bank, half][:])
-                    done(bank)
-                else:
-                    close_bank(bank)
-                    empty(bank, engine)
-
-        run_of(24, "ssvsv")
-        run_of(29, "h")
-        stage_pair("w", 10, "both")
-        stage_pair("wd", 12, "s")
-        quantise("w", 10)
-        stage_pair("w", 12, "v")
-        quantise("wd", 12)
-        quantise("w", 12)
-        run_of(30, "svsvsv")
-        stage_pair("wd", 14, "both")
-        run_of(36, "sv")
-        run_of(38, "h")
-        quantise("wd", 14)
-        stage_pair("w", 14, "v")
-        run_of(39, "ssv")
-        quantise("w", 14)
-        run_of(42, "vsvsv")
-        run_of(47, "h")
+        for pair in range(8, TILES, 2):
+            banks = range(pair * THIRDS, (pair + 2) * THIRDS)
+            for bank in banks:
+                open_bank(bank)
+            for bank, engine in zip(banks, "svsvsv"):
+                close_bank(bank)
+                empty(bank, engine)
+            if pair + 2 < TILES:
+                quantise("w", pair + 2)
+            if pair + 4 < TILES:
+                stage_pair("wd", pair + 4, "v")
+                stage_pair("w", pair + 4, "s")
+                quantise("wd", pair + 4)

@@ -23,7 +23,7 @@ EARLY = EARLY_TILES * P
 DMA_ALIGN = 256
 ROW_BYTES = 4 * T
 EARLY_STORES = (5, 7)
-LATE_STORES = (6, 6, 6, 6, 6, 6)
+LATE_STORES = (4, 5, 7, 7, 7, 6)
 VECTOR_ROWS = 76
 
 

@@ -22,8 +22,8 @@ LATE_TILES = TILES - EARLY_TILES
 EARLY = EARLY_TILES * P
 DMA_ALIGN = 256
 ROW_BYTES = 4 * T
-EARLY_STORES = (5, 7)
-LATE_STORES = (4, 5, 7, 7, 7, 6)
+EARLY_STORES = (3, 4, 5)
+LATE_STORES = (4, 5, 5, 5, 5, 6, 6)
 VECTOR_ROWS = 76
 
 
@@ -39,19 +39,19 @@ def tile_mix_jvp_fm_none_kernel(tc, w, xd, wd, x, out):
         def view(a):
             return a.rearrange("(p j) c -> p j c", j=PACK)
 
-        xd_raw = shared.tile([P, PACK, T], F32, name="xd_raw", align_bytes=DMA_ALIGN, offset=0)
-        nc.sync.dma_start(out=xd_raw[:], in_=view(xd))
-        w_early = keep.tile([P, PACK, EARLY], F32, name="w_early", align_bytes=DMA_ALIGN)
-        nc.scalar.dma_start(out=w_early[:], in_=view(w)[:, :, :EARLY])
-        x_raw = shared.tile([P, PACK, T], F32, name="x_raw", align_bytes=DMA_ALIGN, offset=EARLY_TILES * ROW_BYTES)
+        x_raw = shared.tile([P, PACK, T], F32, name="x_raw", align_bytes=DMA_ALIGN, offset=0)
         nc.sync.dma_start(out=x_raw[:], in_=view(x))
-        wd_raw = keep.tile([P, PACK, N], F32, name="wd_raw", align_bytes=DMA_ALIGN)
-        nc.sync.dma_start(out=wd_raw[:], in_=view(wd))
-        w_late = keep.tile([P, PACK, N - EARLY], F32, name="w_late", align_bytes=DMA_ALIGN)
-        nc.sync.dma_start(out=w_late[:], in_=view(w)[:, :, EARLY:])
+        wd_early = keep.tile([P, PACK, EARLY], F32, name="wd_early", align_bytes=DMA_ALIGN)
+        nc.scalar.dma_start(out=wd_early[:], in_=view(wd)[:, :, :EARLY])
+        xd_raw = shared.tile([P, PACK, T], F32, name="xd_raw", align_bytes=DMA_ALIGN, offset=EARLY_TILES * ROW_BYTES)
+        nc.sync.dma_start(out=xd_raw[:], in_=view(xd))
+        w_raw = keep.tile([P, PACK, N], F32, name="w_raw", align_bytes=DMA_ALIGN)
+        nc.sync.dma_start(out=w_raw[:], in_=view(w))
+        wd_late = keep.tile([P, PACK, N - EARLY], F32, name="wd_late", align_bytes=DMA_ALIGN)
+        nc.sync.dma_start(out=wd_late[:], in_=view(wd)[:, :, EARLY:])
 
         moving = {}
-        for name in ("xd", "x"):
+        for name in ("x", "xd"):
             codes = keep.tile([P, T], U32, name=name + "_codes", align_bytes=64)
             scales = keep.tile([P, T], U8, name=name + "_scales", align_bytes=64)
             moving[name] = (codes, scales)
@@ -84,10 +84,10 @@ def tile_mix_jvp_fm_none_kernel(tc, w, xd, wd, x, out):
 
         def raw_tiles(name, tile, count):
             if tile < EARLY_TILES:
-                slab = w_early[:] if name == "w" else wd_raw[:, :, :EARLY]
+                slab = wd_early[:] if name == "wd" else w_raw[:, :, :EARLY]
                 rows, first = EARLY_TILES, tile
             else:
-                slab = w_late[:] if name == "w" else wd_raw[:, :, EARLY:]
+                slab = wd_late[:] if name == "wd" else w_raw[:, :, EARLY:]
                 rows, first = LATE_TILES, tile - EARLY_TILES
             return slab.rearrange("p j (m r) -> p m j r", r=rows)[:, :, :, first : first + count]
 
@@ -166,10 +166,10 @@ def tile_mix_jvp_fm_none_kernel(tc, w, xd, wd, x, out):
             )
 
         def first_name(bank):
-            return "w" if bank < early_banks else "wd"
+            return "wd" if bank < early_banks else "w"
 
         def second_name(bank):
-            return "wd" if bank < early_banks else "w"
+            return "w" if bank < early_banks else "wd"
 
         def open_bank(bank):
             one_pass(first_name(bank), bank, True, False)
@@ -201,42 +201,42 @@ def tile_mix_jvp_fm_none_kernel(tc, w, xd, wd, x, out):
                 if bank in run and all(b in finished for b in run):
                     store(run.start, run.stop)
 
-        thirds = [stage_moving(xd_raw, c, engine) for c, engine in enumerate("vsv")]
+        thirds = [stage_moving(x_raw, c, engine) for c, engine in enumerate("vsv")]
         for c in (0, 2, 1):
-            quantise_moving("xd", thirds, c)
+            quantise_moving("x", thirds, c)
         for pair in (2, 0):
-            stage_pair("w", pair, "s")
-        thirds = [stage_moving(x_raw, c, "v") for c in range(THIRDS)]
-        quantise_moving("x", thirds, 0)
-        quantise("w", 2)
-        quantise("w", 0)
-        quantise_moving("x", thirds, 1)
-        quantise_moving("x", thirds, 2)
+            stage_pair("wd", pair, "s")
+        thirds = [stage_moving(xd_raw, c, "v") for c in range(THIRDS)]
+        quantise_moving("xd", thirds, 0)
+        quantise("wd", 2)
+        quantise("wd", 0)
+        quantise_moving("xd", thirds, 1)
+        quantise_moving("xd", thirds, 2)
         for bank in reversed(parks):
             park(bank, "s")
         for bank in held:
             open_bank(bank)
 
-        stage_pair("wd", 0, "both")
-        stage_pair("wd", 2, "s")
-        quantise("wd", 0, 1)
-        quantise("wd", 1, 1)
-        stage_pair("wd", 6, "v")
+        stage_pair("w", 0, "both")
+        stage_pair("w", 2, "s")
+        quantise("w", 0, 1)
+        quantise("w", 1, 1)
+        stage_pair("w", 6, "v")
         for bank, engine in zip(held, "vsvsssss"):
             close_bank(bank)
             if bank < 6:
                 empty(bank, engine)
             if bank == 0:
-                quantise("wd", 2)
-                quantise("wd", 6)
+                quantise("w", 2)
+                quantise("w", 6)
             if bank == 2:
-                stage_pair("wd", 4, "v")
+                stage_pair("w", 4, "v")
         for bank in parks:
             close_bank(bank)
         empty(8, "v")
         empty(6, "s")
         empty(7, "s")
-        quantise("wd", 4)
+        quantise("w", 4)
         empty(9, "v")
         park(23, "s")
         empty(10, "v")
@@ -246,27 +246,27 @@ def tile_mix_jvp_fm_none_kernel(tc, w, xd, wd, x, out):
         for bank in (18, 19, 12, 13, 14, 15, 16, 17):
             open_bank(bank)
 
-        stage_pair("w", 4, "both")
-        stage_pair("w", 6, "s")
-        quantise("w", 4, 1)
-        quantise("w", 5, 1)
-        stage_pair("wd", 8, "v")
+        stage_pair("wd", 4, "both")
+        stage_pair("wd", 6, "s")
+        quantise("wd", 4, 1)
+        quantise("wd", 5, 1)
+        stage_pair("w", 8, "v")
         for bank, engine in zip(range(12, 20), "vsvsvsvs"):
             close_bank(bank)
             empty(bank, engine)
             if bank == 12:
-                quantise("w", 6)
-        quantise("wd", 8)
-        stage_pair("w", 8, "v")
+                quantise("wd", 6)
+        quantise("w", 8)
+        stage_pair("wd", 8, "v")
         open_bank(20)
         for bank, engine in zip(range(20, 24), "svvv"):
             close_bank(bank)
             empty(bank, engine)
             if bank == 21:
-                quantise("w", 8)
-        stage_pair("wd", 10, "s")
+                quantise("wd", 8)
         stage_pair("w", 10, "s")
-        quantise("wd", 10)
+        stage_pair("wd", 10, "s")
+        quantise("w", 10)
         for pair in range(8, TILES, 2):
             banks = range(pair * THIRDS, (pair + 2) * THIRDS)
             for bank in banks:
@@ -275,8 +275,8 @@ def tile_mix_jvp_fm_none_kernel(tc, w, xd, wd, x, out):
                 close_bank(bank)
                 empty(bank, engine)
             if pair + 2 < TILES:
-                quantise("w", pair + 2)
+                quantise("wd", pair + 2)
             if pair + 4 < TILES:
-                stage_pair("wd", pair + 4, "v")
-                stage_pair("w", pair + 4, "s")
-                quantise("wd", pair + 4)
+                stage_pair("w", pair + 4, "v")
+                stage_pair("wd", pair + 4, "s")
+                quantise("w", pair + 4)

@@ -102,17 +102,16 @@ def tile_mix_jvp_fm_none_kernel(tc, w, xd, wd, x, out):
             else:
                 copy(engine, dst, src)
             staged[name, tile] = s[:].rearrange("p i m j -> p (i m j)")
-            staged[name, tile + 1] = staged[name, tile][:, P * PACK :]
 
-        def quantise(name, tile, count=2):
-            codes = keep.tile([P, count * P], U32, name="%s_codes%d" % (name, tile), align_bytes=64)
-            scales = keep.tile([P, count * P], U8, name="%s_scales%d" % (name, tile), align_bytes=64)
+        def quantise(name, tile):
+            codes = keep.tile([P, 2 * P], U32, name="%s_codes%d" % (name, tile), align_bytes=64)
+            scales = keep.tile([P, 2 * P], U8, name="%s_scales%d" % (name, tile), align_bytes=64)
             nc.vector.quantize_mx(
                 out=codes[:].bitcast(fmt[name]),
                 scales=scales[:],
-                in_=staged[name, tile][:, : count * P * PACK],
+                in_=staged[name, tile],
             )
-            for i in range(count):
+            for i in range(2):
                 mx[name, tile + i] = (codes[:, i * P : (i + 1) * P], scales[:, i * P : (i + 1) * P])
 
         early_banks = EARLY_TILES * THIRDS
@@ -219,8 +218,7 @@ def tile_mix_jvp_fm_none_kernel(tc, w, xd, wd, x, out):
 
         stage_pair("w", 0, "both")
         stage_pair("w", 2, "s")
-        quantise("w", 0, 1)
-        quantise("w", 1, 1)
+        quantise("w", 0)
         stage_pair("w", 6, "v")
         for bank, engine in zip(held, "vsvsssss"):
             close_bank(bank)
@@ -248,8 +246,7 @@ def tile_mix_jvp_fm_none_kernel(tc, w, xd, wd, x, out):
 
         stage_pair("wd", 4, "both")
         stage_pair("wd", 6, "s")
-        quantise("wd", 4, 1)
-        quantise("wd", 5, 1)
+        quantise("wd", 4)
         stage_pair("w", 8, "v")
         for bank, engine in zip(range(12, 20), "vsvsvsvs"):
             close_bank(bank)

@@ -268,7 +268,7 @@ def tile_mix_jvp_fm_none_kernel(tc, w, xd, wd, x, out):
             banks = range(pair * THIRDS, (pair + 2) * THIRDS)
             for bank in banks:
                 open_bank(bank)
-            for bank, engine in zip(banks, "svsvsv"):
+            for bank, engine in zip(banks, "svsvsv" if pair + 2 < TILES else "vsvvsv"):
                 close_bank(bank)
                 empty(bank, engine)
             if pair + 2 < TILES:

from contextlib import ExitStack

import concourse.mybir as mybir

K, N, T = 512, 2048, 1536
FLOPS = 2 * 2 * K * N * T

F32 = mybir.dt.float32
BF16 = mybir.dt.bfloat16
U32 = mybir.dt.uint32
U8 = mybir.dt.uint8
E4M3 = mybir.dt.float8_e4m3fn_x4
E5M2 = mybir.dt.float8_e5m2_x4

P = 128
PACK = 4
BANK = 512
THIRDS = T // BANK
TILES = N // P
EARLY_TILES = 4
LATE_TILES = TILES - EARLY_TILES
EARLY = EARLY_TILES * P
DMA_ALIGN = 256
ROW_BYTES = 4 * T
EARLY_STORES = (3, 4, 5)
LATE_STORES = (4, 5, 5, 5, 5, 6, 6)
VECTOR_ROWS = 76


def tile_mix_jvp_fm_none_kernel(tc, w, xd, wd, x, out):
    nc = tc.nc
    with ExitStack() as ctx:
        shared = ctx.enter_context(tc.tile_pool(name="shared", bufs=1))
        keep = ctx.enter_context(tc.tile_pool(name="keep", bufs=1))
        stage = ctx.enter_context(tc.tile_pool(name="stage", bufs=3))
        psum = ctx.enter_context(tc.psum_pool(name="psum", bufs=1))
        ctx.enter_context(tc.manual_schedule())

        def view(a):
            return a.rearrange("(p j) c -> p j c", j=PACK)

        x_raw = shared.tile([P, PACK, T], F32, name="x_raw", align_bytes=DMA_ALIGN, offset=0)
        nc.sync.dma_start(out=x_raw[:], in_=view(x))
        wd_early = keep.tile([P, PACK, EARLY], F32, name="wd_early", align_bytes=DMA_ALIGN)
        nc.scalar.dma_start(out=wd_early[:], in_=view(wd)[:, :, :EARLY])
        xd_raw = shared.tile([P, PACK, T], F32, name="xd_raw", align_bytes=DMA_ALIGN, offset=EARLY_TILES * ROW_BYTES)
        nc.sync.dma_start(out=xd_raw[:], in_=view(xd))
        w_raw = keep.tile([P, PACK, N], F32, name="w_raw", align_bytes=DMA_ALIGN)
        nc.sync.dma_start(out=w_raw[:], in_=view(w))
        wd_late = keep.tile([P, PACK, N - EARLY], F32, name="wd_late", align_bytes=DMA_ALIGN)
        nc.sync.dma_start(out=wd_late[:], in_=view(wd)[:, :, EARLY:])

        moving = {}
        for name in ("x", "xd"):
            codes = keep.tile([P, T], U32, name=name + "_codes", align_bytes=64)
            scales = keep.tile([P, T], U8, name=name + "_scales", align_bytes=64)
            moving[name] = (codes, scales)
        fmt = {"w": E4M3, "x": E4M3, "wd": E5M2, "xd": E5M2}
        partner = {"w": "xd", "wd": "x"}

        def copy(engine, dst, src):
            if engine == "v":
                nc.vector.tensor_copy(out=dst, in_=src)
            else:
                nc.scalar.copy(out=dst, in_=src)

        def stage_moving(raw, c, engine):
            g = stage.tile([P, BANK, PACK], BF16, name="moving", align_bytes=64)
            copy(
                engine,
                g[:].rearrange("p (c i) j -> p c j i", i=4),
                raw[:, :, c * BANK : (c + 1) * BANK].rearrange("p j (c i) -> p c j i", i=4),
            )
            return g

        def quantise_moving(name, staged_thirds, c):
            codes, scales = moving[name]
            cols = slice(c * BANK, (c + 1) * BANK)
            nc.vector.quantize_mx(
                out=codes[:, cols].bitcast(fmt[name]),
                scales=scales[:, cols],
                in_=staged_thirds[c][:].rearrange("p c j -> p (c j)"),
            )

        def raw_tiles(name, tile, count):
            if tile < EARLY_TILES:
                slab = wd_early[:] if name == "wd" else w_raw[:, :, :EARLY]
                rows, first = EARLY_TILES, tile
            else:
                slab = wd_late[:] if name == "wd" else w_raw[:, :, EARLY:]
                rows, first = LATE_TILES, tile - EARLY_TILES
            return slab.rearrange("p j (m r) -> p m j r", r=rows)[:, :, :, first : first + count]

        staged, mx = {}, {}

        def stage_pair(name, tile, engine):
            s = stage.tile([P, 2, P, PACK], BF16, name="weights", bufs=4, align_bytes=64)
            dst, src = s[:].rearrange("p i m j -> p m j i"), raw_tiles(name, tile, 2)
            if engine == "both":
                copy("v", dst[:, :VECTOR_ROWS], src[:, :VECTOR_ROWS])
                copy("s", dst[:, VECTOR_ROWS:], src[:, VECTOR_ROWS:])
            else:
                copy(engine, dst, src)
            staged[name, tile] = s[:].rearrange("p i m j -> p (i m j)")

        def quantise(name, tile):
            codes = keep.tile([P, 2 * P], U32, name="%s_codes%d" % (name, tile), align_bytes=64)
            scales = keep.tile([P, 2 * P], U8, name="%s_scales%d" % (name, tile), align_bytes=64)
            nc.vector.quantize_mx(
                out=codes[:].bitcast(fmt[name]),
                scales=scales[:],
                in_=staged[name, tile],
            )
            for i in range(2):
                mx[name, tile + i] = (codes[:, i * P : (i + 1) * P], scales[:, i * P : (i + 1) * P])

        early_banks = EARLY_TILES * THIRDS
        held = range(8)
        parks = range(8, early_banks)
        slabs = {}

        def slab(late):
            if late not in slabs:
                slabs[late] = shared.tile(
                    [P, (LATE_TILES if late else EARLY_TILES) * T],
                    F32,
                    name="late_result" if late else "early_result",
                    align_bytes=DMA_ALIGN,
                    offset=EARLY_TILES * ROW_BYTES if late else 0,
                )
            return slabs[late]

        def result(first, last):
            late = first >= early_banks
            base = early_banks if late else 0
            return slab(late)[:, (first - base) * BANK : (last - base) * BANK]

        def store(first, last):
            late = first >= early_banks
            base = early_banks if late else 0
            rows = out[EARLY:, :] if late else out[:EARLY, :]
            flat = rows.rearrange("(m r) t -> m (r t)", m=P)
            nc.sync.dma_start(out=flat[:, (first - base) * BANK : (last - base) * BANK], in_=result(first, last))

        acc, parked, slot = {}, set(), {}
        free = list(range(8))

        def one_pass(name, bank, start, stop):
            tile, c = divmod(bank, THIRDS)
            codes, scales = mx[name, tile]
            other_codes, other_scales = moving[partner[name]]
            if start:
                slot[bank] = free[0]
                free.remove(slot[bank])
                acc[bank] = psum.tile([P, BANK], F32, name="acc%d" % slot[bank])
            cols = slice(c * BANK, (c + 1) * BANK)
            nc.tensor.matmul_mx(
                out=acc[bank][:],
                lhsT=codes.bitcast(fmt[name]),
                lhsT_scale=scales,
                rhs=other_codes[:, cols].bitcast(fmt[partner[name]]),
                rhs_scale=other_scales[:, cols],
                start=start,
                stop=stop,
            )

        def first_name(bank):
            return "wd" if bank < early_banks else "w"

        def second_name(bank):
            return "w" if bank < early_banks else "wd"

        def open_bank(bank):
            one_pass(first_name(bank), bank, True, False)

        def park(bank, engine):
            one_pass(first_name(bank), bank, True, True)
            copy(engine, result(bank, bank + 1), acc[bank][:])
            parked.add(bank)
            free.append(slot[bank])

        runs, total = [], 0
        for size in EARLY_STORES + LATE_STORES:
            runs.append(range(total, total + size))
            total = total + size
        finished = set()

        def close_bank(bank):
            one_pass(second_name(bank), bank, bank in parked, True)

        def empty(bank, engine):
            free.append(slot[bank])
            if bank in parked:
                target = result(bank, bank + 1)
                nc.vector.tensor_tensor(out=target, in0=acc[bank][:], in1=target, op=mybir.AluOpType.add)
            else:
                copy(engine, result(bank, bank + 1), acc[bank][:])
            finished.add(bank)
            for run in runs:
                if bank in run and all(b in finished for b in run):
                    store(run.start, run.stop)

        thirds = [stage_moving(x_raw, c, engine) for c, engine in enumerate("vsv")]
        for c in (0, 2, 1):
            quantise_moving("x", thirds, c)
        for pair in (2, 0):
            stage_pair("wd", pair, "s")
        thirds = [stage_moving(xd_raw, c, "v") for c in range(THIRDS)]
        quantise_moving("xd", thirds, 0)
        quantise("wd", 2)
        quantise("wd", 0)
        quantise_moving("xd", thirds, 1)
        quantise_moving("xd", thirds, 2)
        for bank in reversed(parks):
            park(bank, "s")
        for bank in held:
            open_bank(bank)

        stage_pair("w", 0, "both")
        stage_pair("w", 2, "s")
        quantise("w", 0)
        stage_pair("w", 6, "v")
        for bank, engine in zip(held, "vsvsssss"):
            close_bank(bank)
            if bank < 6:
                empty(bank, engine)
            if bank == 0:
                quantise("w", 2)
                quantise("w", 6)
            if bank == 2:
                stage_pair("w", 4, "v")
        for bank in parks:
            close_bank(bank)
        empty(8, "v")
        empty(6, "s")
        empty(7, "s")
        quantise("w", 4)
        empty(9, "v")
        park(23, "s")
        empty(10, "v")
        park(22, "s")
        empty(11, "v")
        park(21, "s")
        for bank in (18, 19, 12, 13, 14, 15, 16, 17):
            open_bank(bank)

        stage_pair("wd", 4, "both")
        stage_pair("wd", 6, "s")
        quantise("wd", 4)
        stage_pair("w", 8, "v")
        for bank, engine in zip(range(12, 20), "vsvsvsvs"):
            close_bank(bank)
            empty(bank, engine)
            if bank == 12:
                quantise("wd", 6)
        quantise("w", 8)
        stage_pair("wd", 8, "v")
        open_bank(20)
        for bank, engine in zip(range(20, 24), "svvv"):
            close_bank(bank)
            empty(bank, engine)
            if bank == 21:
                quantise("wd", 8)
        stage_pair("w", 10, "s")
        stage_pair("wd", 10, "s")
        quantise("w", 10)
        for pair in range(8, TILES, 2):
            banks = range(pair * THIRDS, (pair + 2) * THIRDS)
            for bank in banks:
                open_bank(bank)
            for bank, engine in zip(banks, "svsvsv" if pair + 2 < TILES else "vsvvsv"):
                close_bank(bank)
                empty(bank, engine)
            if pair + 2 < TILES:
                quantise("wd", pair + 2)
            if pair + 4 < TILES:
                stage_pair("w", pair + 4, "v")
                stage_pair("wd", pair + 4, "s")
                quantise("w", pair + 4)
